import numpy as np
import ml_dtypes


def mxq(x, axis, fmt="e4m3"):
    dtype, down = {"e4m3": (ml_dtypes.float8_e4m3fn, 7), "e5m2": (ml_dtypes.float8_e5m2, 14)}[fmt]
    v = np.moveaxis(np.asarray(x, np.float32).astype(ml_dtypes.bfloat16).astype(np.float64), axis, -1)
    blocks = v.reshape(v.shape[:-1] + (-1, 32))
    amax = np.abs(blocks).max(-1, keepdims=True)
    byte = np.maximum(np.where(amax > 0, np.frexp(amax)[1] - 1 + 127, 0) - down, 1)
    scale = np.exp2(byte - 127.0)
    codes = (blocks / scale).astype(np.float32).astype(dtype).astype(np.float64)
    return np.moveaxis((codes * scale).reshape(v.shape), -1, axis)


WIDE = False


def mx_kscale(k):
    if not WIDE:
        return np.ones(k)
    levels = np.array([10, -10, 5, -5, 0])
    if k % 512:
        return np.exp2(np.random.permutation(np.resize(levels, k // 32))).repeat(32)
    a = np.empty((k // 512, 16))
    for p in range(k // 512):
        a[p, :8] = np.random.permutation(np.resize(levels, 8))
        for g in range(8):
            far = levels[np.abs(levels - a[p, g]) >= 10]
            a[p, g + 8] = far[np.random.randint(len(far))]
    return np.exp2(a.ravel()).repeat(32)


BF16 = ml_dtypes.bfloat16


def bf(x):
    return np.asarray(x, np.float32).astype(BF16)


def f64(x):
    return np.asarray(x).astype(np.float64)


E2M1 = np.array([0.0, 0.5, 1.0, 1.5, 2.0, 3.0, 4.0, 6.0, -0.0, -0.5, -1.0, -1.5, -2.0, -3.0, -4.0, -6.0])


def pack_weight(w, fmt):
    k, n = w.shape
    w = f64(bf(w)).reshape(k // 32, 32, n)
    amax = np.abs(w).max(1)
    if fmt == "e4m3":
        byte = np.frexp(amax)[1] - 1 + 127 - 7
    else:
        mant, ex = np.frexp(amax / 6.0)
        byte = np.where(mant > 0.5, ex, ex - 1) + 127
    byte = np.clip(np.where(amax > 0, byte, 1), 1, 254)
    scaled = (w * np.exp2(127.0 - byte)[:, None, :]).reshape(k, n).astype(np.float32)
    by_word = np.ascontiguousarray(scaled.reshape(k // 512, 128, 4, n).transpose(0, 1, 3, 2))
    if fmt == "e4m3":
        words = by_word.astype(ml_dtypes.float8_e4m3fn).view(np.uint8)
    else:
        c = by_word.astype(ml_dtypes.float4_e2m1fn).view(np.uint8) & 0xF
        words = c[..., 0::2] | (c[..., 1::2] << 4)
    return np.ascontiguousarray(words), np.ascontiguousarray(byte.astype(np.uint8).reshape(k // 512, 16, n))


def unpack_weight(words, scales, fmt):
    g, p, n, _ = words.shape
    if fmt == "e4m3":
        vals = np.ascontiguousarray(words).view(ml_dtypes.float8_e4m3fn).astype(np.float64)
    else:
        nib = np.empty((g, p, n, 4), np.uint8)
        nib[..., 0::2] = words & 0xF
        nib[..., 1::2] = words >> 4
        vals = E2M1[nib]
    vals = vals * np.repeat(np.exp2(scales.astype(np.float64) - 127.0), 8, axis=1)[..., None]
    return vals.transpose(0, 1, 3, 2).reshape(g * 512, n)
def pack4(w):
    words, scales = pack_weight(w, "e2m1")
    return words.reshape(words.shape[0], 128, -1), scales


def unpack4(words, scales):
    return unpack_weight(words.reshape(words.shape[0], 128, -1, 2), scales, "e2m1")


R, D, L, S = 1024, 1536, 1024, 512


def draw0():
    s, t, u = mx_kscale(D), mx_kscale(L), mx_kscale(R)
    b = np.random.standard_normal((D, L)) / np.sqrt(D)
    spread_words, spread_scales = pack4(b.T / t[:, None])
    return {"force": bf(np.random.standard_normal((R, D)) * s * u[:, None]),
            "root": bf(b / s[:, None] * t),
            "noise": bf(0.8 * np.random.standard_normal((R, L)) * u[:, None] * t),
            "spread_words": spread_words,
            "spread_scales": spread_scales,
            "obs": bf(np.random.standard_normal((S, R)) / np.sqrt(R) / u),
            "dt": bf((1 + 0.1 * np.random.standard_normal(R)) / u),
            "tau": bf((1 + 0.1 * np.random.standard_normal(L)) / t)}


def core(force, root, noise, spread_words, spread_scales, obs, dt, tau):
    w = unpack4(spread_words, spread_scales)
    h = mxq(f64(force), 1, "e4m3") @ mxq(f64(root), 0, "e4m3")
    y = h + f64(noise)
    dx = mxq(y, 1, "e4m3") @ w
    dx = dx * f64(dt)[:, None]
    c = mxq(f64(obs), 1, "e4m3") @ mxq(y, 0, "e4m3")
    c = c * f64(tau)
    return dx, c


def e4m3fn_bytes(y):
    return np.clip(np.asarray(y, np.float64), -448.0, 448.0).astype(np.float32).astype(ml_dtypes.float8_e4m3fn).view(np.uint8)


def e4m3fn_values(b):
    return np.asarray(b, np.uint8).view(ml_dtypes.float8_e4m3fn).astype(np.float64)


def setup_inputs():
    d = draw0()
    x0 = np.asarray(d['obs']).astype(np.float64)
    s = (np.max(np.abs(x0), axis=(0,), keepdims=True) / 448.0).astype(np.float32)
    out = {}
    for k, v in d.items():
        if k == 'obs':
            out['obs_bytes'] = e4m3fn_bytes(x0 / s.astype(np.float64))
            out['obs_scale'] = s
        else:
            out[k] = v
    return out


def reference(force, root, noise, spread_words, spread_scales, obs_bytes, obs_scale, dt, tau):
    return core(force, root, noise, spread_words, spread_scales, e4m3fn_values(obs_bytes) * obs_scale.astype(np.float64), dt, tau)

@@ -1,0 +1,348 @@
+from contextlib import ExitStack
+
+import concourse.mybir as mybir
+from concourse.masks import make_identity
+
+R, D, L, S = 1024, 1536, 1024, 512
+P = 128
+FLOPS = 2 * R * D * L + 2 * R * L * D + 2 * S * R * L
+
+F32 = mybir.dt.float32
+BF16 = mybir.dt.bfloat16
+U32 = mybir.dt.uint32
+I32 = mybir.dt.int32
+U8 = mybir.dt.uint8
+FP8 = mybir.dt.float8_e4m3fn
+FP8X4 = mybir.dt.float8_e4m3fn_x4
+FP4X4 = mybir.dt.float4_e2m1fn_x4
+ADD = mybir.AluOpType.add
+MULT = mybir.AluOpType.mult
+COPY = mybir.ActivationFunctionType.Copy
+
+
+def tile_brownian_mobility_step_s8_kernel(
+    tc, force, root, noise, spread_words, spread_scales, obs_bytes, obs_scale, dt, tau, out_0, out_1
+):
+    nc = tc.nc
+    with ExitStack() as ctx:
+        ctx.enter_context(tc.manual_schedule())
+        keep = ctx.enter_context(tc.tile_pool(name="keep", bufs=1))
+        psum = ctx.enter_context(tc.psum_pool(name="psum", bufs=1))
+
+        def sb(shape, dtype, name):
+            return keep.tile(shape, dtype, name=name, tag=name, align_bytes=64)
+
+        def bank_t(shape):
+            return psum.tile(shape, F32, name="turn", tag="turn", bufs=3)
+
+        def bank_a():
+            return psum.tile([P, 512], F32, name="acc", tag="acc", bufs=5)
+
+        ident = sb([P, P], F32, "ident")
+        make_identity(nc, ident[:])
+        wsc = sb([P, 2, D], U8, "wsc")
+        nc.vector.memset(wsc[:].rearrange("p g n -> p (g n)").bitcast(I32), 0)
+        dt_b = sb([P, 8], BF16, "dt_b")
+        nc.gpsimd.dma_start(
+            out=dt_b[:].rearrange("p (g t) -> p g t", t=4), in_=dt.rearrange("(g p t) -> p g t", p=P, t=4)
+        )
+        dt_f = sb([P, 8], F32, "dt_f")
+        nc.gpsimd.tensor_copy(out=dt_f[:], in_=dt_b[:])
+        scale_bc = sb([P, R], F32, "scale_bc")
+        tau_bc = sb([P, L], BF16, "tau_bc")
+
+        f_raw = [[sb([P, 2, D], BF16, f"f_raw{g}{a}") for a in range(2)] for g in range(2)]
+        r_raw = [[sb([P, 4, 512], BF16, f"r_raw{h}{p}") for p in range(3)] for h in range(2)]
+        n_raw = [sb([P, 4, L], BF16, f"n_raw{g}") for g in range(2)]
+        o_bytes = sb([P, 4 * R], U8, "o_bytes")
+        w = sb([P, 2, 2 * D], U8, "w")
+
+        def rows4(x, g):
+            return x[512 * g : 512 * (g + 1), :].rearrange("(p t) d -> p t d", t=4)
+
+        def load_f(g, a, split=False):
+            src = rows4(force, g)
+            if split:
+                for b in range(2):
+                    nc.sync.dma_start(out=f_raw[g][a][:, b, :], in_=src[:, 2 * a + b, :])
+            else:
+                nc.sync.dma_start(out=f_raw[g][a][:], in_=src[:, 2 * a : 2 * a + 2, :])
+
+        def load_r(h, p):
+            nc.sync.dma_start(out=r_raw[h][p][:], in_=rows4(root, p)[:, :, 512 * h : 512 * (h + 1)])
+
+        def load_n(g):
+            nc.sync.dma_start(out=n_raw[g][:], in_=rows4(noise, g))
+
+        load_f(0, 0, split=True)
+        load_f(0, 1)
+        load_r(0, 0)
+        load_r(0, 1)
+        load_f(1, 0)
+        load_f(1, 1)
+        load_r(0, 2)
+        load_r(1, 0)
+        load_n(0)
+        load_r(1, 1)
+        load_r(1, 2)
+        load_n(1)
+        for q in range(4):
+            nc.sync.dma_start(
+                out=wsc[32 * q : 32 * q + 4, :, :].bitcast(I32),
+                in_=spread_scales[:, 4 * q : 4 * q + 4, :].rearrange("g q n -> q g n").bitcast(I32),
+            )
+        nc.sync.dma_start(out=o_bytes[:], in_=obs_bytes.rearrange("(p i) r -> p (i r)", i=4))
+        nc.sync.dma_start(out=scale_bc[:], in_=obs_scale.rearrange("o r -> (o r)").partition_broadcast(P))
+        nc.sync.dma_start(out=w[:].bitcast(I32), in_=spread_words.rearrange("g p b -> p g b").bitcast(I32))
+        nc.sync.dma_start(out=tau_bc[:], in_=tau.partition_broadcast(P))
+
+        f_codes = [sb([P, 3, 512], U32, f"f_codes{g}") for g in range(2)]
+        f_sc = [sb([P, 3, 512], U8, f"f_sc{g}") for g in range(2)]
+        r_codes = [[sb([P, 512], U32, f"r_codes{h}{p}") for p in range(3)] for h in range(2)]
+        r_sc = [[sb([P, 512], U8, f"r_sc{h}{p}") for p in range(3)] for h in range(2)]
+        y = [[sb([P, 4, 512], BF16, f"y{g}{h}") for h in range(2)] for g in range(2)]
+        yi_codes = [[sb([P, 512], U32, f"yi_codes{g}{h}") for h in range(2)] for g in range(2)]
+        yi_sc = [[sb([P, 512], U8, f"yi_sc{g}{h}") for h in range(2)] for g in range(2)]
+        yt_codes = [[sb([P, 256], U32, f"yt_codes{g}{t}") for t in range(4)] for g in range(2)]
+        yt_sc = [[sb([P, 256], U8, f"yt_sc{g}{t}") for t in range(4)] for g in range(2)]
+        o_codes = [sb([P, 256], U32, f"o_codes{i}") for i in range(4)]
+        o_sc = [sb([P, 256], U8, f"o_sc{i}") for i in range(4)]
+
+        def copy(engine, out, in_):
+            if engine == "v":
+                nc.vector.tensor_copy(out=out, in_=in_)
+            else:
+                nc.scalar.copy(out=out, in_=in_)
+
+        turned = {}
+
+        def turn(key, pieces, step):
+            xt = bank_t([P, 2, 2, P])
+            for a in range(2):
+                src, k0 = pieces[a]
+                for u in range(2):
+                    k = k0 + (u if step == 2 else P * u)
+                    nc.tensor.transpose(xt[:, a, u, :], src[:, k : k + (P - 1) * step + 1 : step], ident[:])
+            tx = keep.tile([P, 1024], BF16, name="turned", tag="turned", bufs=6, align_bytes=64)
+            nc.scalar.copy(
+                out=tx[:].bitcast(F32).rearrange("p (a r u) -> p a r u", a=2, u=2),
+                in_=xt[:].rearrange("p a u r -> p a r u"),
+            )
+            turned[key] = tx
+
+        def quant(key, codes, sc):
+            nc.vector.quantize_mx(out=codes.bitcast(FP8X4), scales=sc, in_=turned[key][:])
+
+        def ft(g, a):
+            words = f_raw[g][a][:].rearrange("p t d -> p (t d)").bitcast(F32)
+            for p in range(3):
+                turn(("f", g, a, p), [(words, b * (D // 2) + 256 * p) for b in range(2)], 2)
+
+        def fq(g, a):
+            cols = slice(256 * a, 256 * a + 256)
+            for p in range(3):
+                quant(("f", g, a, p), f_codes[g][:, p, cols], f_sc[g][:, p, cols])
+
+        def inter(key, engine, src):
+            ix = keep.tile([P, 512, 4], BF16, name="inter", tag="inter", bufs=4, align_bytes=64)
+            if engine == "v":
+                nc.vector.tensor_copy(out=ix[:], in_=src)
+            else:
+                nc.scalar.copy(out=ix[:], in_=src)
+            turned[key] = ix
+
+        def inter_quant(key, codes, sc):
+            nc.vector.quantize_mx(
+                out=codes[:].bitcast(FP8X4), scales=sc[:], in_=turned[key][:].rearrange("p w j -> p (w j)")
+            )
+
+        def ri(h, p, engine):
+            inter(("r", h, p), engine, r_raw[h][p][:].rearrange("p j w -> p w j"))
+
+        def rq(h, p):
+            inter_quant(("r", h, p), r_codes[h][p], r_sc[h][p])
+
+        accs = {}
+
+        def s1(g, h, a):
+            for t in (2 * a, 2 * a + 1):
+                accs[g, h, t] = bank_a()
+            for p in range(3):
+                for t in (2 * a, 2 * a + 1):
+                    cols = slice(128 * t, 128 * t + 128)
+                    nc.tensor.matmul_mx(
+                        out=accs[g, h, t][:],
+                        lhsT=f_codes[g][:, p, cols].bitcast(FP8X4),
+                        lhsT_scale=f_sc[g][:, p, cols],
+                        rhs=r_codes[h][p][:].bitcast(FP8X4),
+                        rhs_scale=r_sc[h][p][:],
+                        start=(p == 0),
+                        stop=(p == 2),
+                    )
+
+        def ya(g, h, a):
+            for t in (2 * a, 2 * a + 1):
+                nc.vector.tensor_tensor(
+                    out=y[g][h][:, t, :].rearrange("p (u k e) -> p u k e", u=2, e=2),
+                    in0=accs[g, h, t][:].rearrange("p (k u e) -> p u k e", u=2, e=2),
+                    in1=n_raw[g][:, t, 512 * h : 512 * h + 512].rearrange("p (k u e) -> p u k e", u=2, e=2),
+                    op=ADD,
+                )
+
+        def yi(g, h, engine):
+            inter(("y", g, h), engine, y[g][h][:].rearrange("p t c -> p c t"))
+
+        def yq(g, h):
+            inter_quant(("y", g, h), yi_codes[g][h], yi_sc[g][h])
+
+        def yt(g, a):
+            for t in (2 * a, 2 * a + 1):
+                turn(
+                    ("yt", g, t),
+                    [(y[g][h][:].rearrange("p t c -> p (t c)").bitcast(F32), 256 * t) for h in range(2)],
+                    1,
+                )
+
+        def yk(g, a):
+            for t in (2 * a, 2 * a + 1):
+                quant(("yt", g, t), yt_codes[g][t][:], yt_sc[g][t][:])
+
+        o_x = sb([P, 4 * R], BF16, "o_x")
+
+        def ox(a):
+            for i in (2 * a, 2 * a + 1):
+                cols = slice(R * i, R * (i + 1))
+                nc.vector.tensor_tensor(out=o_x[:, cols], in0=o_bytes[:, cols].bitcast(FP8), in1=scale_bc[:], op=MULT)
+
+        def ot(a):
+            words = o_x[:].bitcast(F32)
+            for i in (2 * a, 2 * a + 1):
+                turn(("o", i), [(words, 512 * i + 256 * g) for g in range(2)], 2)
+
+        def oq(a):
+            for i in (2 * a, 2 * a + 1):
+                quant(("o", i), o_codes[i][:], o_sc[i][:])
+
+        def s2(g, t, on_vector=()):
+            dx = keep.tile([P, D], F32, name="dx", tag="dx", bufs=4, align_bytes=64)
+            step = dt_f[:, 4 * g + t : 4 * g + t + 1]
+            for n in range(3):
+                acc = bank_a()
+                for h in range(2):
+                    nc.tensor.matmul_mx(
+                        out=acc[:],
+                        lhsT=yt_codes[g][t][:, 128 * h : 128 * h + 128].bitcast(FP8X4),
+                        lhsT_scale=yt_sc[g][t][:, 128 * h : 128 * h + 128],
+                        rhs=w[:, h, 1024 * n : 1024 * n + 1024].bitcast(FP4X4),
+                        rhs_scale=wsc[:, h, 512 * n : 512 * n + 512],
+                        start=(h == 0),
+                        stop=(h == 1),
+                    )
+                out = dx[:, 512 * n : 512 * n + 512]
+                if n in on_vector:
+                    nc.vector.tensor_scalar(out=out, in0=acc[:], scalar1=step, scalar2=None, op0=MULT)
+                else:
+                    nc.scalar.activation(out=out, in_=acc[:], func=COPY, scale=step)
+            nc.sync.dma_start(out=rows4(out_0, g)[:, t, :], in_=dx[:])
+
+        def s3(h, a):
+            for i in (2 * a, 2 * a + 1):
+                acc = bank_a()
+                accs["c", h, i] = acc
+                for g in range(2):
+                    nc.tensor.matmul_mx(
+                        out=acc[:],
+                        lhsT=o_codes[i][:, 128 * g : 128 * g + 128].bitcast(FP8X4),
+                        lhsT_scale=o_sc[i][:, 128 * g : 128 * g + 128],
+                        rhs=yi_codes[g][h][:].bitcast(FP8X4),
+                        rhs_scale=yi_sc[g][h][:],
+                        start=(g == 0),
+                        stop=(g == 1),
+                    )
+
+        def co(h, a):
+            cols = slice(512 * h, 512 * h + 512)
+            for i in (2 * a, 2 * a + 1):
+                c = keep.tile([P, 512], F32, name="c", tag="c", bufs=4, align_bytes=64)
+                nc.vector.tensor_tensor(
+                    out=c[:].rearrange("p (k u e) -> p k u e", u=2, e=2),
+                    in0=accs["c", h, i][:].rearrange("p (u k e) -> p k u e", u=2, e=2),
+                    in1=tau_bc[:, cols].rearrange("p (k u e) -> p k u e", u=2, e=2),
+                    op=MULT,
+                )
+                nc.sync.dma_start(out=out_1.rearrange("(p i) l -> p i l", i=4)[:, i, cols], in_=c[:])
+
+        ft(0, 0)
+        ft(0, 1)
+        fq(0, 0)
+        ri(0, 0, "s")
+        fq(0, 1)
+        ft(1, 0)
+        ri(0, 1, "v")
+        rq(0, 1)
+        rq(0, 0)
+        fq(1, 0)
+        ri(0, 2, "v")
+        ft(1, 1)
+        rq(0, 2)
+        s1(0, 0, 0)
+        fq(1, 1)
+        ya(0, 0, 0)
+        ri(1, 0, "s")
+        s1(0, 0, 1)
+        rq(1, 0)
+        ya(0, 0, 1)
+        s1(1, 0, 0)
+        ri(1, 1, "s")
+        ri(1, 2, "v")
+        yi(0, 0, "s")
+        rq(1, 1)
+        ya(1, 0, 0)
+        rq(1, 2)
+        s1(1, 0, 1)
+        ya(1, 0, 1)
+        s1(0, 1, 0)
+        yi(1, 0, "s")
+        s1(0, 1, 1)
+        yq(0, 0)
+        ya(0, 1, 0)
+        yt(0, 0)
+        ya(0, 1, 1)
+        s1(1, 1, 0)
+        yk(0, 0)
+        ox(0)
+        ya(1, 1, 0)
+        s1(1, 1, 1)
+        yq(1, 0)
+        yi(0, 1, "s")
+        yt(0, 1)
+        yk(0, 1)
+        ya(1, 1, 1)
+        ot(0)
+        yt(1, 0)
+        oq(0)
+        yk(1, 0)
+        yq(0, 1)
+        s2(0, 0)
+        yt(1, 1)
+        s2(0, 1)
+        yk(1, 1)
+        ox(1)
+        yi(1, 1, "v")
+        s2(0, 2)
+        s2(0, 3)
+        yq(1, 1)
+        s3(0, 0)
+        co(0, 0)
+        s2(1, 0, on_vector=(0,))
+        s2(1, 1, on_vector=(0,))
+        s2(1, 2, on_vector=(0,))
+        s2(1, 3, on_vector=(0,))
+        ot(1)
+        oq(1)
+        s3(1, 0)
+        co(1, 0)
+        s3(0, 1)
+        co(0, 1)
+        s3(1, 1)
+        co(1, 1)

@@ -40,6 +40,8 @@ def tile_brownian_mobility_step_s8_kernel(
 
         ident = sb([P, P], F32, "ident")
         make_identity(nc, ident[:])
+        warm = sb([P, 512], BF16, "warm")
+        nc.vector.memset(warm[:], 0.0)
         wsc = sb([P, 2, D], U8, "wsc")
         nc.vector.memset(wsc[:].rearrange("p g n -> p (g n)").bitcast(I32), 0)
         dt_b = sb([P, 8], BF16, "dt_b")
@@ -74,27 +76,42 @@ def tile_brownian_mobility_step_s8_kernel(
         def load_n(g):
             nc.sync.dma_start(out=n_raw[g][:], in_=rows4(noise, g))
 
-        load_f(0, 0, split=True)
-        load_f(0, 1)
+        def load_wsc():
+            for q in range(4):
+                nc.sync.dma_start(
+                    out=wsc[32 * q : 32 * q + 4, :, :].bitcast(I32),
+                    in_=spread_scales[:, 4 * q : 4 * q + 4, :].rearrange("g q n -> q g n").bitcast(I32),
+                )
+
+        def load_o():
+            nc.sync.dma_start(out=o_bytes[:], in_=obs_bytes.rearrange("(p i) r -> p (i r)", i=4))
+
+        def load_scb():
+            nc.sync.dma_start(out=scale_bc[:], in_=obs_scale.rearrange("o r -> (o r)").partition_broadcast(P))
+
+        def load_w():
+            nc.sync.dma_start(out=w[:].bitcast(I32), in_=spread_words.rearrange("g p b -> p g b").bitcast(I32))
+
+        def load_tau():
+            nc.sync.dma_start(out=tau_bc[:], in_=tau.partition_broadcast(P))
+
         load_r(0, 0)
+        load_f(0, 0, split=True)
         load_r(0, 1)
-        load_f(1, 0)
-        load_f(1, 1)
+        load_f(0, 1)
         load_r(0, 2)
+        load_f(1, 0)
         load_r(1, 0)
+        load_f(1, 1)
         load_n(0)
         load_r(1, 1)
         load_r(1, 2)
         load_n(1)
-        for q in range(4):
-            nc.sync.dma_start(
-                out=wsc[32 * q : 32 * q + 4, :, :].bitcast(I32),
-                in_=spread_scales[:, 4 * q : 4 * q + 4, :].rearrange("g q n -> q g n").bitcast(I32),
-            )
-        nc.sync.dma_start(out=o_bytes[:], in_=obs_bytes.rearrange("(p i) r -> p (i r)", i=4))
-        nc.sync.dma_start(out=scale_bc[:], in_=obs_scale.rearrange("o r -> (o r)").partition_broadcast(P))
-        nc.sync.dma_start(out=w[:].bitcast(I32), in_=spread_words.rearrange("g p b -> p g b").bitcast(I32))
-        nc.sync.dma_start(out=tau_bc[:], in_=tau.partition_broadcast(P))
+        load_o()
+        load_scb()
+        load_wsc()
+        load_tau()
+        load_w()
 
         f_codes = [sb([P, 3, 512], U32, f"f_codes{g}") for g in range(2)]
         f_sc = [sb([P, 3, 512], U8, f"f_sc{g}") for g in range(2)]
@@ -164,21 +181,25 @@ def tile_brownian_mobility_step_s8_kernel(
 
         accs = {}
 
-        def s1(g, h, a):
+        def s1(g, h, a, p):
             for t in (2 * a, 2 * a + 1):
-                accs[g, h, t] = bank_a()
-            for p in range(3):
-                for t in (2 * a, 2 * a + 1):
-                    cols = slice(128 * t, 128 * t + 128)
-                    nc.tensor.matmul_mx(
-                        out=accs[g, h, t][:],
-                        lhsT=f_codes[g][:, p, cols].bitcast(FP8X4),
-                        lhsT_scale=f_sc[g][:, p, cols],
-                        rhs=r_codes[h][p][:].bitcast(FP8X4),
-                        rhs_scale=r_sc[h][p][:],
-                        start=(p == 0),
-                        stop=(p == 2),
-                    )
+                if p == 0:
+                    accs[g, h, t] = bank_a()
+                cols = slice(128 * t, 128 * t + 128)
+                nc.tensor.matmul_mx(
+                    out=accs[g, h, t][:],
+                    lhsT=f_codes[g][:, p, cols].bitcast(FP8X4),
+                    lhsT_scale=f_sc[g][:, p, cols],
+                    rhs=r_codes[h][p][:].bitcast(FP8X4),
+                    rhs_scale=r_sc[h][p][:],
+                    start=(p == 0),
+                    stop=(p == 2),
+                )
+
+        def warm_up():
+            acc = bank_a()
+            for k in range(2):
+                nc.tensor.matmul(acc[:], warm[:, 0:P], warm[:], start=True, stop=True)
 
         def ya(g, h, a):
             for t in (2 * a, 2 * a + 1):
@@ -272,68 +293,88 @@ def tile_brownian_mobility_step_s8_kernel(
                 )
                 nc.sync.dma_start(out=out_1.rearrange("(p i) l -> p i l", i=4)[:, i, cols], in_=c[:])
 
+        ri(0, 0, "v")
+        warm_up()
+        warm_up()
+        warm_up()
+        warm_up()
+        rq(0, 0)
         ft(0, 0)
-        ft(0, 1)
+        ri(0, 1, "v")
         fq(0, 0)
-        ri(0, 0, "s")
+        rq(0, 1)
+        warm_up()
+        warm_up()
+        s1(0, 0, 0, 0)
+        ft(0, 1)
+        ri(0, 2, "v")
+        s1(0, 0, 0, 1)
         fq(0, 1)
         ft(1, 0)
-        ri(0, 1, "v")
-        rq(0, 1)
-        rq(0, 0)
-        fq(1, 0)
-        ri(0, 2, "v")
-        ft(1, 1)
         rq(0, 2)
-        s1(0, 0, 0)
-        fq(1, 1)
-        ya(0, 0, 0)
-        ri(1, 0, "s")
-        s1(0, 0, 1)
+        s1(0, 0, 1, 0)
+        ft(1, 1)
+        ri(1, 0, "v")
+        fq(1, 0)
+        s1(0, 0, 0, 2)
         rq(1, 0)
-        ya(0, 0, 1)
-        s1(1, 0, 0)
+        s1(0, 0, 1, 1)
+        fq(1, 1)
         ri(1, 1, "s")
+        ya(0, 0, 0)
+        s1(0, 0, 1, 2)
+        s1(1, 0, 0, 0)
+        s1(1, 0, 0, 1)
+        ya(0, 0, 1)
         ri(1, 2, "v")
-        yi(0, 0, "s")
+        s1(1, 0, 1, 0)
         rq(1, 1)
+        s1(1, 0, 0, 2)
         ya(1, 0, 0)
+        s1(1, 0, 1, 1)
         rq(1, 2)
-        s1(1, 0, 1)
+        s1(1, 0, 1, 2)
+        s1(0, 1, 0, 0)
         ya(1, 0, 1)
-        s1(0, 1, 0)
-        yi(1, 0, "s")
-        s1(0, 1, 1)
-        yq(0, 0)
-        ya(0, 1, 0)
-        yt(0, 0)
-        ya(0, 1, 1)
-        s1(1, 1, 0)
-        yk(0, 0)
+        s1(0, 1, 0, 1)
+        s1(0, 1, 1, 0)
+        s1(0, 1, 0, 2)
+        yi(0, 0, "s")
         ox(0)
-        ya(1, 1, 0)
-        s1(1, 1, 1)
-        yq(1, 0)
-        yi(0, 1, "s")
-        yt(0, 1)
-        yk(0, 1)
-        ya(1, 1, 1)
+        s1(0, 1, 1, 1)
+        ya(0, 1, 0)
+        s1(0, 1, 1, 2)
+        ya(0, 1, 1)
+        yi(1, 0, "s")
         ot(0)
-        yt(1, 0)
+        yt(0, 0)
+        s1(1, 1, 0, 0)
+        s1(1, 1, 1, 0)
+        s1(1, 1, 0, 1)
+        yq(1, 0)
+        s1(1, 1, 1, 1)
         oq(0)
+        yi(0, 1, "s")
+        s1(1, 1, 0, 2)
+        yk(0, 0)
+        yq(0, 0)
+        ya(1, 1, 0)
+        s1(1, 1, 1, 2)
+        ya(1, 1, 1)
+        yt(0, 1)
+        ox(1)
+        s2(0, 0, on_vector=(2,))
+        yt(1, 0)
+        yk(0, 1)
         yk(1, 0)
         yq(0, 1)
-        s2(0, 0)
+        s2(0, 1, on_vector=(2,))
         yt(1, 1)
-        s2(0, 1)
         yk(1, 1)
-        ox(1)
-        yi(1, 1, "v")
         s2(0, 2)
-        s2(0, 3)
+        yi(1, 1, "v")
         yq(1, 1)
-        s3(0, 0)
-        co(0, 0)
+        s2(0, 3)
         s2(1, 0, on_vector=(0,))
         s2(1, 1, on_vector=(0,))
         s2(1, 2, on_vector=(0,))
@@ -341,8 +382,10 @@ def tile_brownian_mobility_step_s8_kernel(
         ot(1)
         oq(1)
         s3(1, 0)
+        s3(0, 0)
         co(1, 0)
-        s3(0, 1)
-        co(0, 1)
         s3(1, 1)
+        co(0, 0)
+        s3(0, 1)
         co(1, 1)
+        co(0, 1)

@@ -53,8 +53,14 @@ def tile_brownian_mobility_step_s8_kernel(
         scale_bc = sb([P, R], F32, "scale_bc")
         tau_bc = sb([P, L], BF16, "tau_bc")
 
-        f_raw = [[sb([P, 2, D], BF16, f"f_raw{g}{a}") for a in range(2)] for g in range(2)]
-        r_raw = [[sb([P, 4, 512], BF16, f"r_raw{h}{p}") for p in range(3)] for h in range(2)]
+        def big(shape, dtype, name):
+            return keep.tile(shape, dtype, name=name, tag="big", bufs=8, align_bytes=64)
+
+        def mid(shape, dtype, name):
+            return keep.tile(shape, dtype, name=name, tag="mid", bufs=6, align_bytes=64)
+
+        f_raw = [[big([P, 2, D], BF16, f"f_raw{g}{a}") for a in range(2)] for g in range(2)]
+        r_raw = [[mid([P, 4, 512], BF16, f"r_raw{h}{p}") for p in range(3)] for h in range(2)]
         n_raw = [sb([P, 4, L], BF16, f"n_raw{g}") for g in range(2)]
         o_bytes = sb([P, 4 * R], U8, "o_bytes")
         w = sb([P, 2, 2 * D], U8, "w")
@@ -95,23 +101,23 @@ def tile_brownian_mobility_step_s8_kernel(
         def load_tau():
             nc.sync.dma_start(out=tau_bc[:], in_=tau.partition_broadcast(P))
 
-        load_r(0, 0)
         load_f(0, 0, split=True)
-        load_r(0, 1)
         load_f(0, 1)
-        load_r(0, 2)
+        load_r(0, 0)
         load_f(1, 0)
+        load_r(0, 1)
         load_r(1, 0)
         load_f(1, 1)
-        load_n(0)
+        load_r(0, 2)
         load_r(1, 1)
-        load_r(1, 2)
+        load_n(0)
         load_n(1)
+        load_r(1, 2)
         load_o()
         load_scb()
+        load_w()
         load_wsc()
         load_tau()
-        load_w()
 
         f_codes = [sb([P, 3, 512], U32, f"f_codes{g}") for g in range(2)]
         f_sc = [sb([P, 3, 512], U8, f"f_sc{g}") for g in range(2)]
@@ -120,10 +126,10 @@ def tile_brownian_mobility_step_s8_kernel(
         y = [[sb([P, 4, 512], BF16, f"y{g}{h}") for h in range(2)] for g in range(2)]
         yi_codes = [[sb([P, 512], U32, f"yi_codes{g}{h}") for h in range(2)] for g in range(2)]
         yi_sc = [[sb([P, 512], U8, f"yi_sc{g}{h}") for h in range(2)] for g in range(2)]
-        yt_codes = [[sb([P, 256], U32, f"yt_codes{g}{t}") for t in range(4)] for g in range(2)]
-        yt_sc = [[sb([P, 256], U8, f"yt_sc{g}{t}") for t in range(4)] for g in range(2)]
-        o_codes = [sb([P, 256], U32, f"o_codes{i}") for i in range(4)]
-        o_sc = [sb([P, 256], U8, f"o_sc{i}") for i in range(4)]
+        yt_codes = [[sb([P, 512], U32, f"yt_codes{g}{a}") for a in range(2)] for g in range(2)]
+        yt_sc = [[sb([P, 512], U8, f"yt_sc{g}{a}") for a in range(2)] for g in range(2)]
+        o_codes = [sb([P, 512], U32, f"o_codes{a}") for a in range(2)]
+        o_sc = [sb([P, 512], U8, f"o_sc{a}") for a in range(2)]
 
         def copy(engine, out, in_):
             if engine == "v":
@@ -133,19 +139,21 @@ def tile_brownian_mobility_step_s8_kernel(
 
         turned = {}
 
-        def turn(key, pieces, step):
+        def turn(out, pieces, step):
             xt = bank_t([P, 2, 2, P])
             for a in range(2):
                 src, k0 = pieces[a]
                 for u in range(2):
                     k = k0 + (u if step == 2 else P * u)
                     nc.tensor.transpose(xt[:, a, u, :], src[:, k : k + (P - 1) * step + 1 : step], ident[:])
-            tx = keep.tile([P, 1024], BF16, name="turned", tag="turned", bufs=6, align_bytes=64)
             nc.scalar.copy(
-                out=tx[:].bitcast(F32).rearrange("p (a r u) -> p a r u", a=2, u=2),
+                out=out.bitcast(F32).rearrange("p (a r u) -> p a r u", a=2, u=2),
                 in_=xt[:].rearrange("p a u r -> p a r u"),
             )
-            turned[key] = tx
+
+        def turned_pair(key):
+            turned[key] = keep.tile([P, 2048], BF16, name="pair", tag="pair", bufs=4, align_bytes=64)
+            return turned[key]
 
         def quant(key, codes, sc):
             nc.vector.quantize_mx(out=codes.bitcast(FP8X4), scales=sc, in_=turned[key][:])
@@ -153,7 +161,9 @@ def tile_brownian_mobility_step_s8_kernel(
         def ft(g, a):
             words = f_raw[g][a][:].rearrange("p t d -> p (t d)").bitcast(F32)
             for p in range(3):
-                turn(("f", g, a, p), [(words, b * (D // 2) + 256 * p) for b in range(2)], 2)
+                tx = keep.tile([P, 1024], BF16, name="turned", tag="turned", bufs=6, align_bytes=64)
+                turned["f", g, a, p] = tx
+                turn(tx[:], [(words, b * (D // 2) + 256 * p) for b in range(2)], 2)
 
         def fq(g, a):
             cols = slice(256 * a, 256 * a + 256)
@@ -162,10 +172,12 @@ def tile_brownian_mobility_step_s8_kernel(
 
         def inter(key, engine, src):
             ix = keep.tile([P, 512, 4], BF16, name="inter", tag="inter", bufs=4, align_bytes=64)
+            out = ix[:].rearrange("p (c i) j -> p c j i", i=4)
+            src = src.rearrange("p j (c i) -> p c j i", i=4)
             if engine == "v":
-                nc.vector.tensor_copy(out=ix[:], in_=src)
+                nc.vector.tensor_copy(out=out, in_=src)
             else:
-                nc.scalar.copy(out=ix[:], in_=src)
+                nc.scalar.copy(out=out, in_=src)
             turned[key] = ix
 
         def inter_quant(key, codes, sc):
@@ -174,7 +186,7 @@ def tile_brownian_mobility_step_s8_kernel(
             )
 
         def ri(h, p, engine):
-            inter(("r", h, p), engine, r_raw[h][p][:].rearrange("p j w -> p w j"))
+            inter(("r", h, p), engine, r_raw[h][p][:])
 
         def rq(h, p):
             inter_quant(("r", h, p), r_codes[h][p], r_sc[h][p])
@@ -211,22 +223,23 @@ def tile_brownian_mobility_step_s8_kernel(
                 )
 
         def yi(g, h, engine):
-            inter(("y", g, h), engine, y[g][h][:].rearrange("p t c -> p c t"))
+            inter(("y", g, h), engine, y[g][h][:])
 
         def yq(g, h):
             inter_quant(("y", g, h), yi_codes[g][h], yi_sc[g][h])
 
         def yt(g, a):
-            for t in (2 * a, 2 * a + 1):
+            pair = turned_pair(("yt", g, a))
+            for b in range(2):
+                t = 2 * a + b
                 turn(
-                    ("yt", g, t),
+                    pair[:, 1024 * b : 1024 * b + 1024],
                     [(y[g][h][:].rearrange("p t c -> p (t c)").bitcast(F32), 256 * t) for h in range(2)],
                     1,
                 )
 
         def yk(g, a):
-            for t in (2 * a, 2 * a + 1):
-                quant(("yt", g, t), yt_codes[g][t][:], yt_sc[g][t][:])
+            quant(("yt", g, a), yt_codes[g][a][:], yt_sc[g][a][:])
 
         o_x = sb([P, 4 * R], BF16, "o_x")
 
@@ -237,23 +250,25 @@ def tile_brownian_mobility_step_s8_kernel(
 
         def ot(a):
             words = o_x[:].bitcast(F32)
-            for i in (2 * a, 2 * a + 1):
-                turn(("o", i), [(words, 512 * i + 256 * g) for g in range(2)], 2)
+            pair = turned_pair(("o", a))
+            for b in range(2):
+                k0 = 512 * (2 * a + b)
+                turn(pair[:, 1024 * b : 1024 * b + 1024], [(words, k0 + 256 * g) for g in range(2)], 2)
 
         def oq(a):
-            for i in (2 * a, 2 * a + 1):
-                quant(("o", i), o_codes[i][:], o_sc[i][:])
+            quant(("o", a), o_codes[a][:], o_sc[a][:])
 
         def s2(g, t, on_vector=()):
-            dx = keep.tile([P, D], F32, name="dx", tag="dx", bufs=4, align_bytes=64)
+            dx = big([P, D], F32, f"dx{g}{t}")
             step = dt_f[:, 4 * g + t : 4 * g + t + 1]
             for n in range(3):
                 acc = bank_a()
                 for h in range(2):
+                    m = slice(256 * (t % 2) + 128 * h, 256 * (t % 2) + 128 * h + 128)
                     nc.tensor.matmul_mx(
                         out=acc[:],
-                        lhsT=yt_codes[g][t][:, 128 * h : 128 * h + 128].bitcast(FP8X4),
-                        lhsT_scale=yt_sc[g][t][:, 128 * h : 128 * h + 128],
+                        lhsT=yt_codes[g][t // 2][:, m].bitcast(FP8X4),
+                        lhsT_scale=yt_sc[g][t // 2][:, m],
                         rhs=w[:, h, 1024 * n : 1024 * n + 1024].bitcast(FP4X4),
                         rhs_scale=wsc[:, h, 512 * n : 512 * n + 512],
                         start=(h == 0),
@@ -271,10 +286,11 @@ def tile_brownian_mobility_step_s8_kernel(
                 acc = bank_a()
                 accs["c", h, i] = acc
                 for g in range(2):
+                    m = slice(256 * (i % 2) + 128 * g, 256 * (i % 2) + 128 * g + 128)
                     nc.tensor.matmul_mx(
                         out=acc[:],
-                        lhsT=o_codes[i][:, 128 * g : 128 * g + 128].bitcast(FP8X4),
-                        lhsT_scale=o_sc[i][:, 128 * g : 128 * g + 128],
+                        lhsT=o_codes[i // 2][:, m].bitcast(FP8X4),
+                        lhsT_scale=o_sc[i // 2][:, m],
                         rhs=yi_codes[g][h][:].bitcast(FP8X4),
                         rhs_scale=yi_sc[g][h][:],
                         start=(g == 0),
@@ -283,109 +299,110 @@ def tile_brownian_mobility_step_s8_kernel(
 
         def co(h, a):
             cols = slice(512 * h, 512 * h + 512)
+            pair = mid([P, 2, 512], F32, f"c{h}{a}")
             for i in (2 * a, 2 * a + 1):
-                c = keep.tile([P, 512], F32, name="c", tag="c", bufs=4, align_bytes=64)
+                c = pair[:, i % 2, :]
                 nc.vector.tensor_tensor(
-                    out=c[:].rearrange("p (k u e) -> p k u e", u=2, e=2),
+                    out=c.rearrange("p (k u e) -> p k u e", u=2, e=2),
                     in0=accs["c", h, i][:].rearrange("p (u k e) -> p k u e", u=2, e=2),
                     in1=tau_bc[:, cols].rearrange("p (k u e) -> p k u e", u=2, e=2),
                     op=MULT,
                 )
-                nc.sync.dma_start(out=out_1.rearrange("(p i) l -> p i l", i=4)[:, i, cols], in_=c[:])
+                nc.sync.dma_start(out=out_1.rearrange("(p i) l -> p i l", i=4)[:, i, cols], in_=c)
 
+        warm_up()
+        warm_up()
+        warm_up()
+        warm_up()
         ri(0, 0, "v")
-        warm_up()
-        warm_up()
-        warm_up()
-        warm_up()
-        rq(0, 0)
         ft(0, 0)
-        ri(0, 1, "v")
-        fq(0, 0)
-        rq(0, 1)
         warm_up()
-        warm_up()
-        s1(0, 0, 0, 0)
         ft(0, 1)
-        ri(0, 2, "v")
-        s1(0, 0, 0, 1)
-        fq(0, 1)
+        fq(0, 0)
         ft(1, 0)
-        rq(0, 2)
+        rq(0, 0)
+        fq(0, 1)
+        s1(0, 0, 0, 0)
+        ri(0, 1, "v")
+        warm_up()
         s1(0, 0, 1, 0)
-        ft(1, 1)
-        ri(1, 0, "v")
+        rq(0, 1)
         fq(1, 0)
-        s1(0, 0, 0, 2)
-        rq(1, 0)
+        s1(0, 0, 0, 1)
+        ri(1, 0, "s")
+        ri(0, 2, "v")
+        ft(1, 1)
         s1(0, 0, 1, 1)
+        rq(1, 0)
+        rq(0, 2)
         fq(1, 1)
+        s1(0, 0, 0, 2)
         ri(1, 1, "s")
-        ya(0, 0, 0)
-        s1(0, 0, 1, 2)
         s1(1, 0, 0, 0)
+        s1(0, 0, 1, 2)
+        ya(0, 0, 0)
         s1(1, 0, 0, 1)
         ya(0, 0, 1)
-        ri(1, 2, "v")
-        s1(1, 0, 1, 0)
-        rq(1, 1)
         s1(1, 0, 0, 2)
-        ya(1, 0, 0)
+        ri(1, 2, "s")
+        rq(1, 1)
+        s1(1, 0, 1, 0)
         s1(1, 0, 1, 1)
-        rq(1, 2)
+        ya(1, 0, 0)
         s1(1, 0, 1, 2)
         s1(0, 1, 0, 0)
         ya(1, 0, 1)
-        s1(0, 1, 0, 1)
         s1(0, 1, 1, 0)
-        s1(0, 1, 0, 2)
-        yi(0, 0, "s")
-        ox(0)
+        s1(0, 1, 0, 1)
+        rq(1, 2)
         s1(0, 1, 1, 1)
-        ya(0, 1, 0)
+        ox(0)
+        s1(0, 1, 0, 2)
         s1(0, 1, 1, 2)
-        ya(0, 1, 1)
         yi(1, 0, "s")
         ot(0)
-        yt(0, 0)
+        ya(0, 1, 0)
         s1(1, 1, 0, 0)
+        ya(0, 1, 1)
+        yt(0, 0)
+        yi(0, 0, "s")
         s1(1, 1, 1, 0)
         s1(1, 1, 0, 1)
-        yq(1, 0)
-        s1(1, 1, 1, 1)
-        oq(0)
-        yi(0, 1, "s")
-        s1(1, 1, 0, 2)
-        yk(0, 0)
-        yq(0, 0)
-        ya(1, 1, 0)
-        s1(1, 1, 1, 2)
-        ya(1, 1, 1)
-        yt(0, 1)
         ox(1)
-        s2(0, 0, on_vector=(2,))
-        yt(1, 0)
+        yk(0, 0)
+        s1(1, 1, 1, 1)
+        s1(1, 1, 0, 2)
+        yt(0, 1)
+        s1(1, 1, 1, 2)
+        ya(1, 1, 0)
+        yq(1, 0)
+        ya(1, 1, 1)
         yk(0, 1)
+        s2(0, 0)
+        yi(0, 1, "v")
+        yt(1, 0)
+        s2(0, 1)
         yk(1, 0)
-        yq(0, 1)
-        s2(0, 1, on_vector=(2,))
+        yq(0, 0)
+        oq(0)
         yt(1, 1)
-        yk(1, 1)
         s2(0, 2)
+        yq(0, 1)
+        yk(1, 1)
         yi(1, 1, "v")
-        yq(1, 1)
         s2(0, 3)
-        s2(1, 0, on_vector=(0,))
-        s2(1, 1, on_vector=(0,))
-        s2(1, 2, on_vector=(0,))
-        s2(1, 3, on_vector=(0,))
+        s2(1, 0, on_vector=(2,))
         ot(1)
+        yq(1, 1)
         oq(1)
-        s3(1, 0)
+        s2(1, 1, on_vector=(2,))
+        s2(1, 2, on_vector=(2,))
+        s2(1, 3, on_vector=(2,))
         s3(0, 0)
-        co(1, 0)
-        s3(1, 1)
         co(0, 0)
+        s3(1, 0)
+        co(1, 0)
         s3(0, 1)
-        co(1, 1)
         co(0, 1)
+        s3(1, 1)
+        co(1, 1)

@@ -33,10 +33,10 @@ def tile_brownian_mobility_step_s8_kernel(
             return keep.tile(shape, dtype, name=name, tag=name, align_bytes=64)
 
         def bank_t(shape):
-            return psum.tile(shape, F32, name="turn", tag="turn", bufs=3)
+            return psum.tile(shape, F32, name="turn", tag="turn", bufs=2)
 
         def bank_a():
-            return psum.tile([P, 512], F32, name="acc", tag="acc", bufs=5)
+            return psum.tile([P, 512], F32, name="acc", tag="acc", bufs=6)
 
         ident = sb([P, P], F32, "ident")
         make_identity(nc, ident[:])
@@ -57,10 +57,10 @@ def tile_brownian_mobility_step_s8_kernel(
             return keep.tile(shape, dtype, name=name, tag="big", bufs=8, align_bytes=64)
 
         def mid(shape, dtype, name):
-            return keep.tile(shape, dtype, name=name, tag="mid", bufs=6, align_bytes=64)
+            return keep.tile(shape, dtype, name=name, tag="mid", bufs=3, align_bytes=64)
 
         f_raw = [[big([P, 2, D], BF16, f"f_raw{g}{a}") for a in range(2)] for g in range(2)]
-        r_raw = [[mid([P, 4, 512], BF16, f"r_raw{h}{p}") for p in range(3)] for h in range(2)]
+        r_raw = [mid([P, 4, L], BF16, f"r_raw{p}") for p in range(3)]
         n_raw = [sb([P, 4, L], BF16, f"n_raw{g}") for g in range(2)]
         o_bytes = sb([P, 4 * R], U8, "o_bytes")
         w = sb([P, 2, 2 * D], U8, "w")
@@ -76,8 +76,8 @@ def tile_brownian_mobility_step_s8_kernel(
             else:
                 nc.sync.dma_start(out=f_raw[g][a][:], in_=src[:, 2 * a : 2 * a + 2, :])
 
-        def load_r(h, p):
-            nc.sync.dma_start(out=r_raw[h][p][:], in_=rows4(root, p)[:, :, 512 * h : 512 * (h + 1)])
+        def load_r(p):
+            nc.sync.dma_start(out=r_raw[p][:], in_=rows4(root, p))
 
         def load_n(g):
             nc.sync.dma_start(out=n_raw[g][:], in_=rows4(noise, g))
@@ -102,22 +102,19 @@ def tile_brownian_mobility_step_s8_kernel(
             nc.sync.dma_start(out=tau_bc[:], in_=tau.partition_broadcast(P))
 
         load_f(0, 0, split=True)
+        load_r(0)
         load_f(0, 1)
-        load_r(0, 0)
         load_f(1, 0)
-        load_r(0, 1)
-        load_r(1, 0)
+        load_r(1)
+        load_r(2)
         load_f(1, 1)
-        load_r(0, 2)
-        load_r(1, 1)
         load_n(0)
-        load_n(1)
-        load_r(1, 2)
-        load_o()
         load_scb()
-        load_w()
-        load_wsc()
         load_tau()
+        load_o()
+        load_n(1)
+        load_wsc()
+        load_w()
 
         f_codes = [sb([P, 3, 512], U32, f"f_codes{g}") for g in range(2)]
         f_sc = [sb([P, 3, 512], U8, f"f_sc{g}") for g in range(2)]
@@ -186,7 +183,7 @@ def tile_brownian_mobility_step_s8_kernel(
             )
 
         def ri(h, p, engine):
-            inter(("r", h, p), engine, r_raw[h][p][:])
+            inter(("r", h, p), engine, r_raw[p][:, :, 512 * h : 512 * h + 512])
 
         def rq(h, p):
             inter_quant(("r", h, p), r_codes[h][p], r_sc[h][p])
@@ -258,7 +255,7 @@ def tile_brownian_mobility_step_s8_kernel(
         def oq(a):
             quant(("o", a), o_codes[a][:], o_sc[a][:])
 
-        def s2(g, t, on_vector=()):
+        def s2(g, t, on_vector=(), split=False):
             dx = big([P, D], F32, f"dx{g}{t}")
             step = dt_f[:, 4 * g + t : 4 * g + t + 1]
             for n in range(3):
@@ -279,7 +276,10 @@ def tile_brownian_mobility_step_s8_kernel(
                     nc.vector.tensor_scalar(out=out, in0=acc[:], scalar1=step, scalar2=None, op0=MULT)
                 else:
                     nc.scalar.activation(out=out, in_=acc[:], func=COPY, scale=step)
-            nc.sync.dma_start(out=rows4(out_0, g)[:, t, :], in_=dx[:])
+                if split:
+                    nc.sync.dma_start(out=rows4(out_0, g)[:, t, 512 * n : 512 * n + 512], in_=out)
+            if not split:
+                nc.sync.dma_start(out=rows4(out_0, g)[:, t, :], in_=dx[:])
 
         def s3(h, a):
             for i in (2 * a, 2 * a + 1):
@@ -299,9 +299,10 @@ def tile_brownian_mobility_step_s8_kernel(
 
         def co(h, a):
             cols = slice(512 * h, 512 * h + 512)
-            pair = mid([P, 2, 512], F32, f"c{h}{a}")
+            if a == 0:
+                accs["out", h] = mid([P, 4, 512], F32, f"c{h}")
             for i in (2 * a, 2 * a + 1):
-                c = pair[:, i % 2, :]
+                c = accs["out", h][:, i, :]
                 nc.vector.tensor_tensor(
                     out=c.rearrange("p (k u e) -> p k u e", u=2, e=2),
                     in0=accs["c", h, i][:].rearrange("p (u k e) -> p k u e", u=2, e=2),
@@ -313,96 +314,94 @@ def tile_brownian_mobility_step_s8_kernel(
         warm_up()
         warm_up()
         warm_up()
-        warm_up()
-        ri(0, 0, "v")
         ft(0, 0)
-        warm_up()
-        ft(0, 1)
+        ri(0, 0, "v")
         fq(0, 0)
-        ft(1, 0)
         rq(0, 0)
+        warm_up()
+        ri(1, 0, "v")
+        ft(0, 1)
         fq(0, 1)
+        ft(1, 0)
         s1(0, 0, 0, 0)
         ri(0, 1, "v")
-        warm_up()
         s1(0, 0, 1, 0)
-        rq(0, 1)
-        fq(1, 0)
-        s1(0, 0, 0, 1)
-        ri(1, 0, "s")
-        ri(0, 2, "v")
-        ft(1, 1)
-        s1(0, 0, 1, 1)
-        rq(1, 0)
-        rq(0, 2)
-        fq(1, 1)
-        s1(0, 0, 0, 2)
         ri(1, 1, "s")
-        s1(1, 0, 0, 0)
-        s1(0, 0, 1, 2)
-        ya(0, 0, 0)
-        s1(1, 0, 0, 1)
-        ya(0, 0, 1)
-        s1(1, 0, 0, 2)
-        ri(1, 2, "s")
-        rq(1, 1)
-        s1(1, 0, 1, 0)
-        s1(1, 0, 1, 1)
-        ya(1, 0, 0)
-        s1(1, 0, 1, 2)
+        rq(1, 0)
+        rq(0, 1)
         s1(0, 1, 0, 0)
-        ya(1, 0, 1)
-        s1(0, 1, 1, 0)
-        s1(0, 1, 0, 1)
+        s1(0, 0, 0, 1)
+        ri(0, 2, "v")
+        s1(0, 0, 1, 1)
+        rq(0, 2)
+        fq(1, 0)
+        ri(1, 2, "s")
+        s1(0, 0, 0, 2)
+        s1(0, 0, 1, 2)
+        rq(1, 1)
+        ya(0, 0, 0)
+        ft(1, 1)
         rq(1, 2)
-        s1(0, 1, 1, 1)
-        ox(0)
+        ya(0, 0, 1)
+        s1(0, 1, 0, 1)
+        s1(0, 1, 1, 0)
         s1(0, 1, 0, 2)
-        s1(0, 1, 1, 2)
-        yi(1, 0, "s")
-        ot(0)
+        s1(0, 1, 1, 1)
         ya(0, 1, 0)
-        s1(1, 1, 0, 0)
-        ya(0, 1, 1)
-        yt(0, 0)
+        fq(1, 1)
         yi(0, 0, "s")
-        s1(1, 1, 1, 0)
+        s1(1, 1, 0, 0)
+        s1(0, 1, 1, 2)
+        yt(0, 0)
         s1(1, 1, 0, 1)
-        ox(1)
-        yk(0, 0)
-        s1(1, 1, 1, 1)
+        ya(0, 1, 1)
+        s1(1, 0, 0, 0)
         s1(1, 1, 0, 2)
         yt(0, 1)
-        s1(1, 1, 1, 2)
+        s1(1, 0, 0, 1)
+        yq(0, 0)
+        s1(1, 0, 1, 0)
+        s1(1, 0, 0, 2)
+        yi(0, 1, "s")
         ya(1, 1, 0)
-        yq(1, 0)
-        ya(1, 1, 1)
+        yk(0, 0)
+        s1(1, 0, 1, 1)
         yk(0, 1)
-        s2(0, 0)
-        yi(0, 1, "v")
+        s1(1, 1, 1, 0)
+        ya(1, 0, 0)
+        s1(1, 0, 1, 2)
+        yq(0, 1)
+        ya(1, 0, 1)
+        s1(1, 1, 1, 1)
         yt(1, 0)
+        s1(1, 1, 1, 2)
+        ya(1, 1, 1)
+        s2(0, 0)
+        yi(1, 0, "v")
         s2(0, 1)
         yk(1, 0)
-        yq(0, 0)
-        oq(0)
+        yq(1, 0)
         yt(1, 1)
-        s2(0, 2)
-        yq(0, 1)
-        yk(1, 1)
         yi(1, 1, "v")
+        s2(0, 2)
+        yq(1, 1)
+        yk(1, 1)
+        ox(0)
         s2(0, 3)
         s2(1, 0, on_vector=(2,))
-        ot(1)
-        yq(1, 1)
-        oq(1)
+        ox(1)
         s2(1, 1, on_vector=(2,))
+        ot(0)
+        oq(0)
         s2(1, 2, on_vector=(2,))
         s2(1, 3, on_vector=(2,))
         s3(0, 0)
+        ot(1)
         co(0, 0)
+        oq(1)
         s3(1, 0)
         co(1, 0)
         s3(0, 1)
-        co(0, 1)
         s3(1, 1)
+        co(0, 1)
         co(1, 1)

@@ -5,6 +5,8 @@ from concourse.masks import make_identity
 
 R, D, L, S = 1024, 1536, 1024, 512
 P = 128
+HALF = 512
+K_PASS = 512
 FLOPS = 2 * R * D * L + 2 * R * L * D + 2 * S * R * L
 
 F32 = mybir.dt.float32
@@ -26,382 +28,408 @@ def tile_brownian_mobility_step_s8_kernel(
     nc = tc.nc
     with ExitStack() as ctx:
         ctx.enter_context(tc.manual_schedule())
-        keep = ctx.enter_context(tc.tile_pool(name="keep", bufs=1))
+        sbuf = ctx.enter_context(tc.tile_pool(name="sbuf", bufs=1))
         psum = ctx.enter_context(tc.psum_pool(name="psum", bufs=1))
 
-        def sb(shape, dtype, name):
-            return keep.tile(shape, dtype, name=name, tag=name, align_bytes=64)
+        def own(shape, dtype, name):
+            return sbuf.tile(shape, dtype, name=name, tag=name, align_bytes=64)
 
-        def bank_t(shape):
-            return psum.tile(shape, F32, name="turn", tag="turn", bufs=2)
+        def shared(shape, dtype, name, tag, bufs):
+            return sbuf.tile(shape, dtype, name=name, tag=tag, bufs=bufs, align_bytes=64)
 
-        def bank_a():
-            return psum.tile([P, 512], F32, name="acc", tag="acc", bufs=6)
+        def sums():
+            return psum.tile([P, HALF], F32, name="sums", tag="sums", bufs=6)
 
-        ident = sb([P, P], F32, "ident")
+        ident = own([P, P], F32, "ident")
         make_identity(nc, ident[:])
-        warm = sb([P, 512], BF16, "warm")
-        nc.vector.memset(warm[:], 0.0)
-        wsc = sb([P, 2, D], U8, "wsc")
-        nc.vector.memset(wsc[:].rearrange("p g n -> p (g n)").bitcast(I32), 0)
-        dt_b = sb([P, 8], BF16, "dt_b")
+        zeros = own([P, HALF], BF16, "zeros")
+        nc.vector.memset(zeros[:], 0.0)
+        w_scales = own([P, 2, D], U8, "w_scales")
+        nc.vector.memset(w_scales[:].rearrange("p g n -> p (g n)").bitcast(I32), 0)
+        dt_in = own([P, 8], BF16, "dt_in")
         nc.gpsimd.dma_start(
-            out=dt_b[:].rearrange("p (g t) -> p g t", t=4), in_=dt.rearrange("(g p t) -> p g t", p=P, t=4)
+            out=dt_in[:].rearrange("p (g t) -> p g t", t=4), in_=dt.rearrange("(g p t) -> p g t", p=P, t=4)
         )
-        dt_f = sb([P, 8], F32, "dt_f")
-        nc.gpsimd.tensor_copy(out=dt_f[:], in_=dt_b[:])
-        scale_bc = sb([P, R], F32, "scale_bc")
-        tau_bc = sb([P, L], BF16, "tau_bc")
+        dt_f = own([P, 8], F32, "dt_f")
+        nc.gpsimd.tensor_copy(out=dt_f[:], in_=dt_in[:])
 
-        def big(shape, dtype, name):
-            return keep.tile(shape, dtype, name=name, tag="big", bufs=8, align_bytes=64)
-
-        def mid(shape, dtype, name):
-            return keep.tile(shape, dtype, name=name, tag="mid", bufs=3, align_bytes=64)
-
-        f_raw = [[big([P, 2, D], BF16, f"f_raw{g}{a}") for a in range(2)] for g in range(2)]
-        r_raw = [mid([P, 4, L], BF16, f"r_raw{p}") for p in range(3)]
-        n_raw = [sb([P, 4, L], BF16, f"n_raw{g}") for g in range(2)]
-        o_bytes = sb([P, 4 * R], U8, "o_bytes")
-        w = sb([P, 2, 2 * D], U8, "w")
+        force_in = [[shared([P, 2, D], BF16, f"force{g}{a}", "row", 8) for a in range(2)] for g in range(2)]
+        root_in = [shared([P, 4, L], BF16, f"root{p}", "block", 3) for p in range(3)]
+        noise_in = [own([P, 4, L], BF16, f"noise{g}") for g in range(2)]
+        obs_codes_in = own([P, 4 * R], U8, "obs_codes_in")
+        scale_rows = own([P, R], F32, "scale_rows")
+        tau_rows = own([P, L], BF16, "tau_rows")
+        w = own([P, 2, 2 * D], U8, "w")
 
         def rows4(x, g):
-            return x[512 * g : 512 * (g + 1), :].rearrange("(p t) d -> p t d", t=4)
+            return x[K_PASS * g : K_PASS * (g + 1), :].rearrange("(p t) d -> p t d", t=4)
 
-        def load_f(g, a, split=False):
-            src = rows4(force, g)
-            if split:
-                for b in range(2):
-                    nc.sync.dma_start(out=f_raw[g][a][:, b, :], in_=src[:, 2 * a + b, :])
-            else:
-                nc.sync.dma_start(out=f_raw[g][a][:], in_=src[:, 2 * a : 2 * a + 2, :])
+        def load_force(g, a):
+            nc.sync.dma_start(out=force_in[g][a][:], in_=rows4(force, g)[:, 2 * a : 2 * a + 2, :])
 
-        def load_r(p):
-            nc.sync.dma_start(out=r_raw[p][:], in_=rows4(root, p))
+        def load_root(p):
+            nc.sync.dma_start(out=root_in[p][:], in_=rows4(root, p))
 
-        def load_n(g):
-            nc.sync.dma_start(out=n_raw[g][:], in_=rows4(noise, g))
+        def load_noise(g):
+            nc.sync.dma_start(out=noise_in[g][:], in_=rows4(noise, g))
 
-        def load_wsc():
+        def load_obs():
+            nc.sync.dma_start(out=obs_codes_in[:], in_=obs_bytes.rearrange("(p i) r -> p (i r)", i=4))
+
+        def load_scale():
+            nc.sync.dma_start(out=scale_rows[:], in_=obs_scale.rearrange("o r -> (o r)").partition_broadcast(P))
+
+        def load_tau():
+            nc.sync.dma_start(out=tau_rows[:], in_=tau.partition_broadcast(P))
+
+        def load_w_scales():
             for q in range(4):
                 nc.sync.dma_start(
-                    out=wsc[32 * q : 32 * q + 4, :, :].bitcast(I32),
+                    out=w_scales[32 * q : 32 * q + 4, :, :].bitcast(I32),
                     in_=spread_scales[:, 4 * q : 4 * q + 4, :].rearrange("g q n -> q g n").bitcast(I32),
                 )
-
-        def load_o():
-            nc.sync.dma_start(out=o_bytes[:], in_=obs_bytes.rearrange("(p i) r -> p (i r)", i=4))
-
-        def load_scb():
-            nc.sync.dma_start(out=scale_bc[:], in_=obs_scale.rearrange("o r -> (o r)").partition_broadcast(P))
 
         def load_w():
             nc.sync.dma_start(out=w[:].bitcast(I32), in_=spread_words.rearrange("g p b -> p g b").bitcast(I32))
 
-        def load_tau():
-            nc.sync.dma_start(out=tau_bc[:], in_=tau.partition_broadcast(P))
-
-        load_f(0, 0, split=True)
-        load_r(0)
-        load_f(0, 1)
-        load_f(1, 0)
-        load_r(1)
-        load_r(2)
-        load_f(1, 1)
-        load_n(0)
-        load_scb()
+        for b in range(2):
+            nc.sync.dma_start(out=force_in[0][0][:, b, :], in_=rows4(force, 0)[:, b, :])
+        load_root(0)
+        load_force(0, 1)
+        load_root(1)
+        load_force(1, 0)
+        load_root(2)
+        load_force(1, 1)
+        load_noise(0)
         load_tau()
-        load_o()
-        load_n(1)
-        load_wsc()
+        load_noise(1)
+        load_obs()
+        load_scale()
         load_w()
+        load_w_scales()
 
-        f_codes = [sb([P, 3, 512], U32, f"f_codes{g}") for g in range(2)]
-        f_sc = [sb([P, 3, 512], U8, f"f_sc{g}") for g in range(2)]
-        r_codes = [[sb([P, 512], U32, f"r_codes{h}{p}") for p in range(3)] for h in range(2)]
-        r_sc = [[sb([P, 512], U8, f"r_sc{h}{p}") for p in range(3)] for h in range(2)]
-        y = [[sb([P, 4, 512], BF16, f"y{g}{h}") for h in range(2)] for g in range(2)]
-        yi_codes = [[sb([P, 512], U32, f"yi_codes{g}{h}") for h in range(2)] for g in range(2)]
-        yi_sc = [[sb([P, 512], U8, f"yi_sc{g}{h}") for h in range(2)] for g in range(2)]
-        yt_codes = [[sb([P, 512], U32, f"yt_codes{g}{a}") for a in range(2)] for g in range(2)]
-        yt_sc = [[sb([P, 512], U8, f"yt_sc{g}{a}") for a in range(2)] for g in range(2)]
-        o_codes = [sb([P, 512], U32, f"o_codes{a}") for a in range(2)]
-        o_sc = [sb([P, 512], U8, f"o_sc{a}") for a in range(2)]
+        force_q = [(own([P, 3, 512], U32, f"force_c{g}"), own([P, 3, 512], U8, f"force_s{g}")) for g in range(2)]
+        root_q = [
+            [(own([P, HALF], U32, f"root_c{h}{p}"), own([P, HALF], U8, f"root_s{h}{p}")) for p in range(3)]
+            for h in range(2)
+        ]
+        y = [[own([P, 4, HALF], BF16, f"y{g}{h}") for h in range(2)] for g in range(2)]
+        y_by_replica = [
+            [(own([P, HALF], U32, f"yr_c{g}{h}"), own([P, HALF], U8, f"yr_s{g}{h}")) for h in range(2)]
+            for g in range(2)
+        ]
+        y_by_mode = [
+            [(own([P, 512], U32, f"ym_c{g}{a}"), own([P, 512], U8, f"ym_s{g}{a}")) for a in range(2)]
+            for g in range(2)
+        ]
+        obs_q = [(own([P, 512], U32, f"obs_c{a}"), own([P, 512], U8, f"obs_s{a}")) for a in range(2)]
+        obs = own([P, 4 * R], BF16, "obs")
+        live = {}
 
-        def copy(engine, out, in_):
-            if engine == "v":
-                nc.vector.tensor_copy(out=out, in_=in_)
-            else:
-                nc.scalar.copy(out=out, in_=in_)
+        on_vector = nc.vector.tensor_copy
+        on_scalar = nc.scalar.copy
 
-        turned = {}
+        def quantise(key, codes, scales):
+            nc.vector.quantize_mx(out=codes.bitcast(FP8X4), scales=scales, in_=live[key])
 
-        def turn(out, pieces, step):
-            xt = bank_t([P, 2, 2, P])
-            for a in range(2):
-                src, k0 = pieces[a]
+        def turn(out, blocks, step):
+            bank = psum.tile([P, 2, 2, P], F32, name="turned", tag="turned", bufs=2)
+            for b, (words, first) in enumerate(blocks):
                 for u in range(2):
-                    k = k0 + (u if step == 2 else P * u)
-                    nc.tensor.transpose(xt[:, a, u, :], src[:, k : k + (P - 1) * step + 1 : step], ident[:])
+                    k = first + (u if step == 2 else P * u)
+                    nc.tensor.transpose(bank[:, b, u, :], words[:, k : k + (P - 1) * step + 1 : step], ident[:])
             nc.scalar.copy(
-                out=out.bitcast(F32).rearrange("p (a r u) -> p a r u", a=2, u=2),
-                in_=xt[:].rearrange("p a u r -> p a r u"),
+                out=out.bitcast(F32).rearrange("p (b r u) -> p b r u", b=2, u=2),
+                in_=bank[:].rearrange("p b u r -> p b r u"),
             )
 
-        def turned_pair(key):
-            turned[key] = keep.tile([P, 2048], BF16, name="pair", tag="pair", bufs=4, align_bytes=64)
-            return turned[key]
+        def half_of_pair(key, b):
+            if key not in live:
+                live[key] = shared([P, 2048], BF16, "pair", "pair", 4)[:]
+            return live[key][:, 1024 * b : 1024 * b + 1024]
 
-        def quant(key, codes, sc):
-            nc.vector.quantize_mx(out=codes.bitcast(FP8X4), scales=sc, in_=turned[key][:])
-
-        def ft(g, a):
-            words = f_raw[g][a][:].rearrange("p t d -> p (t d)").bitcast(F32)
-            for p in range(3):
-                tx = keep.tile([P, 1024], BF16, name="turned", tag="turned", bufs=6, align_bytes=64)
-                turned["f", g, a, p] = tx
-                turn(tx[:], [(words, b * (D // 2) + 256 * p) for b in range(2)], 2)
-
-        def fq(g, a):
-            cols = slice(256 * a, 256 * a + 256)
-            for p in range(3):
-                quant(("f", g, a, p), f_codes[g][:, p, cols], f_sc[g][:, p, cols])
-
-        def inter(key, engine, src):
-            ix = keep.tile([P, 512, 4], BF16, name="inter", tag="inter", bufs=4, align_bytes=64)
-            out = ix[:].rearrange("p (c i) j -> p c j i", i=4)
-            src = src.rearrange("p j (c i) -> p c j i", i=4)
-            if engine == "v":
-                nc.vector.tensor_copy(out=out, in_=src)
-            else:
-                nc.scalar.copy(out=out, in_=src)
-            turned[key] = ix
-
-        def inter_quant(key, codes, sc):
-            nc.vector.quantize_mx(
-                out=codes[:].bitcast(FP8X4), scales=sc[:], in_=turned[key][:].rearrange("p w j -> p (w j)")
+        def interleave(key, copy, rows):
+            tile = shared([P, HALF, 4], BF16, "interleaved", "interleaved", 4)
+            copy(
+                out=tile[:].rearrange("p (c i) t -> p c t i", i=4),
+                in_=rows.rearrange("p t (c i) -> p c t i", i=4),
             )
+            live[key] = tile[:].rearrange("p c t -> p (c t)")
 
-        def ri(h, p, engine):
-            inter(("r", h, p), engine, r_raw[p][:, :, 512 * h : 512 * h + 512])
+        def warm_up():
+            bank = sums()
+            for k in range(2):
+                nc.tensor.matmul(bank[:], zeros[:, 0:P], zeros[:], start=True, stop=True)
 
-        def rq(h, p):
-            inter_quant(("r", h, p), r_codes[h][p], r_sc[h][p])
+        def turn_force(g, a, p):
+            words = force_in[g][a][:].rearrange("p t d -> p (t d)").bitcast(F32)
+            tile = shared([P, 1024], BF16, "force_turned", "force_turned", 6)
+            turn(tile[:], [(words, D // 2 * b + 256 * p) for b in range(2)], 2)
+            live["force", g, a, p] = tile[:]
 
-        accs = {}
+        def quantise_force(g, a, p):
+            codes, scales = force_q[g]
+            tiles = slice(256 * a, 256 * a + 256)
+            quantise(("force", g, a, p), codes[:, p, tiles], scales[:, p, tiles])
 
-        def s1(g, h, a, p):
+        def interleave_root(h, p, copy):
+            interleave(("root", h, p), copy, root_in[p][:, :, HALF * h : HALF * h + HALF])
+
+        def quantise_root(h, p):
+            codes, scales = root_q[h][p]
+            quantise(("root", h, p), codes[:], scales[:])
+
+        def modes(g, h, a, p):
+            f_codes, f_scales = force_q[g]
+            r_codes, r_scales = root_q[h][p]
             for t in (2 * a, 2 * a + 1):
                 if p == 0:
-                    accs[g, h, t] = bank_a()
-                cols = slice(128 * t, 128 * t + 128)
+                    live["modes", g, h, t] = sums()
+                m = slice(P * t, P * t + P)
                 nc.tensor.matmul_mx(
-                    out=accs[g, h, t][:],
-                    lhsT=f_codes[g][:, p, cols].bitcast(FP8X4),
-                    lhsT_scale=f_sc[g][:, p, cols],
-                    rhs=r_codes[h][p][:].bitcast(FP8X4),
-                    rhs_scale=r_sc[h][p][:],
+                    out=live["modes", g, h, t][:],
+                    lhsT=f_codes[:, p, m].bitcast(FP8X4),
+                    lhsT_scale=f_scales[:, p, m],
+                    rhs=r_codes[:].bitcast(FP8X4),
+                    rhs_scale=r_scales[:],
                     start=(p == 0),
                     stop=(p == 2),
                 )
 
-        def warm_up():
-            acc = bank_a()
-            for k in range(2):
-                nc.tensor.matmul(acc[:], warm[:, 0:P], warm[:], start=True, stop=True)
+        def add_noise(g, h, t):
+            nc.vector.tensor_tensor(
+                out=y[g][h][:, t, :].rearrange("p (u k e) -> p u k e", u=2, e=2),
+                in0=live["modes", g, h, t][:].rearrange("p (k u e) -> p u k e", u=2, e=2),
+                in1=noise_in[g][:, t, HALF * h : HALF * h + HALF].rearrange("p (k u e) -> p u k e", u=2, e=2),
+                op=ADD,
+            )
 
-        def ya(g, h, a):
-            for t in (2 * a, 2 * a + 1):
-                nc.vector.tensor_tensor(
-                    out=y[g][h][:, t, :].rearrange("p (u k e) -> p u k e", u=2, e=2),
-                    in0=accs[g, h, t][:].rearrange("p (k u e) -> p u k e", u=2, e=2),
-                    in1=n_raw[g][:, t, 512 * h : 512 * h + 512].rearrange("p (k u e) -> p u k e", u=2, e=2),
-                    op=ADD,
-                )
+        def interleave_y(g, h, copy):
+            interleave(("y", g, h), copy, y[g][h][:])
 
-        def yi(g, h, engine):
-            inter(("y", g, h), engine, y[g][h][:])
+        def quantise_y_by_replica(g, h):
+            codes, scales = y_by_replica[g][h]
+            quantise(("y", g, h), codes[:], scales[:])
 
-        def yq(g, h):
-            inter_quant(("y", g, h), yi_codes[g][h], yi_sc[g][h])
+        def turn_y(g, t):
+            halves = [(y[g][h][:].rearrange("p t c -> p (t c)").bitcast(F32), 256 * t) for h in range(2)]
+            turn(half_of_pair(("turned y", g, t // 2), t % 2), halves, 1)
 
-        def yt(g, a):
-            pair = turned_pair(("yt", g, a))
-            for b in range(2):
-                t = 2 * a + b
-                turn(
-                    pair[:, 1024 * b : 1024 * b + 1024],
-                    [(y[g][h][:].rearrange("p t c -> p (t c)").bitcast(F32), 256 * t) for h in range(2)],
-                    1,
-                )
+        def quantise_y_by_mode(g, a):
+            codes, scales = y_by_mode[g][a]
+            quantise(("turned y", g, a), codes[:], scales[:])
 
-        def yk(g, a):
-            quant(("yt", g, a), yt_codes[g][a][:], yt_sc[g][a][:])
-
-        o_x = sb([P, 4 * R], BF16, "o_x")
-
-        def ox(a):
-            for i in (2 * a, 2 * a + 1):
-                cols = slice(R * i, R * (i + 1))
-                nc.vector.tensor_tensor(out=o_x[:, cols], in0=o_bytes[:, cols].bitcast(FP8), in1=scale_bc[:], op=MULT)
-
-        def ot(a):
-            words = o_x[:].bitcast(F32)
-            pair = turned_pair(("o", a))
-            for b in range(2):
-                k0 = 512 * (2 * a + b)
-                turn(pair[:, 1024 * b : 1024 * b + 1024], [(words, k0 + 256 * g) for g in range(2)], 2)
-
-        def oq(a):
-            quant(("o", a), o_codes[a][:], o_sc[a][:])
-
-        def s2(g, t, on_vector=(), split=False):
-            dx = big([P, D], F32, f"dx{g}{t}")
+        def displace(g, t, vector_chunk=None, split=False):
+            dx = shared([P, D], F32, f"dx{g}{t}", "row", 8)
             step = dt_f[:, 4 * g + t : 4 * g + t + 1]
+            codes, scales = y_by_mode[g][t // 2]
             for n in range(3):
-                acc = bank_a()
+                bank = sums()
+                cols = slice(HALF * n, HALF * n + HALF)
                 for h in range(2):
-                    m = slice(256 * (t % 2) + 128 * h, 256 * (t % 2) + 128 * h + 128)
+                    m = slice(256 * (t % 2) + P * h, 256 * (t % 2) + P * h + P)
                     nc.tensor.matmul_mx(
-                        out=acc[:],
-                        lhsT=yt_codes[g][t // 2][:, m].bitcast(FP8X4),
-                        lhsT_scale=yt_sc[g][t // 2][:, m],
-                        rhs=w[:, h, 1024 * n : 1024 * n + 1024].bitcast(FP4X4),
-                        rhs_scale=wsc[:, h, 512 * n : 512 * n + 512],
+                        out=bank[:],
+                        lhsT=codes[:, m].bitcast(FP8X4),
+                        lhsT_scale=scales[:, m],
+                        rhs=w[:, h, 2 * HALF * n : 2 * HALF * (n + 1)].bitcast(FP4X4),
+                        rhs_scale=w_scales[:, h, cols],
                         start=(h == 0),
                         stop=(h == 1),
                     )
-                out = dx[:, 512 * n : 512 * n + 512]
-                if n in on_vector:
-                    nc.vector.tensor_scalar(out=out, in0=acc[:], scalar1=step, scalar2=None, op0=MULT)
+                if n == vector_chunk:
+                    nc.vector.tensor_scalar(out=dx[:, cols], in0=bank[:], scalar1=step, scalar2=None, op0=MULT)
                 else:
-                    nc.scalar.activation(out=out, in_=acc[:], func=COPY, scale=step)
+                    nc.scalar.activation(out=dx[:, cols], in_=bank[:], func=COPY, scale=step)
                 if split:
-                    nc.sync.dma_start(out=rows4(out_0, g)[:, t, 512 * n : 512 * n + 512], in_=out)
+                    nc.sync.dma_start(out=rows4(out_0, g)[:, t, cols], in_=dx[:, cols])
             if not split:
                 nc.sync.dma_start(out=rows4(out_0, g)[:, t, :], in_=dx[:])
 
-        def s3(h, a):
+        def scale_obs(a):
             for i in (2 * a, 2 * a + 1):
-                acc = bank_a()
-                accs["c", h, i] = acc
-                for g in range(2):
-                    m = slice(256 * (i % 2) + 128 * g, 256 * (i % 2) + 128 * g + 128)
-                    nc.tensor.matmul_mx(
-                        out=acc[:],
-                        lhsT=o_codes[i // 2][:, m].bitcast(FP8X4),
-                        lhsT_scale=o_sc[i // 2][:, m],
-                        rhs=yi_codes[g][h][:].bitcast(FP8X4),
-                        rhs_scale=yi_sc[g][h][:],
-                        start=(g == 0),
-                        stop=(g == 1),
-                    )
-
-        def co(h, a):
-            cols = slice(512 * h, 512 * h + 512)
-            if a == 0:
-                accs["out", h] = mid([P, 4, 512], F32, f"c{h}")
-            for i in (2 * a, 2 * a + 1):
-                c = accs["out", h][:, i, :]
+                cols = slice(R * i, R * (i + 1))
                 nc.vector.tensor_tensor(
-                    out=c.rearrange("p (k u e) -> p k u e", u=2, e=2),
-                    in0=accs["c", h, i][:].rearrange("p (u k e) -> p k u e", u=2, e=2),
-                    in1=tau_bc[:, cols].rearrange("p (k u e) -> p k u e", u=2, e=2),
-                    op=MULT,
+                    out=obs[:, cols], in0=obs_codes_in[:, cols].bitcast(FP8), in1=scale_rows[:], op=MULT
                 )
-                nc.sync.dma_start(out=out_1.rearrange("(p i) l -> p i l", i=4)[:, i, cols], in_=c)
+
+        def order_obs(a, copy):
+            if "obs" not in live:
+                live["obs"] = shared([P, 2 * R], F32, "obs_words", "block", 3)
+            words = slice(R * a, R * (a + 1))
+            copy(
+                out=live["obs"][:, words].rearrange("p (b u k) -> p b u k", u=2, k=P),
+                in_=obs[:].bitcast(F32)[:, words].rearrange("p (b k u) -> p b u k", u=2, k=P),
+            )
+
+        def turn_obs(i):
+            turn(half_of_pair(("turned obs", i // 2), i % 2), [(live["obs"], 512 * i + 256 * g) for g in range(2)], 1)
+
+        def quantise_obs(a):
+            codes, scales = obs_q[a]
+            quantise(("turned obs", a), codes[:], scales[:])
+
+        def correlate(h, i):
+            bank = sums()
+            codes, scales = obs_q[i // 2]
+            for g in range(2):
+                m = slice(256 * (i % 2) + P * g, 256 * (i % 2) + P * g + P)
+                y_codes, y_scales = y_by_replica[g][h]
+                nc.tensor.matmul_mx(
+                    out=bank[:],
+                    lhsT=codes[:, m].bitcast(FP8X4),
+                    lhsT_scale=scales[:, m],
+                    rhs=y_codes[:].bitcast(FP8X4),
+                    rhs_scale=y_scales[:],
+                    start=(g == 0),
+                    stop=(g == 1),
+                )
+            live["correlation", h, i] = bank
+
+        def store_c(h, i):
+            if ("c", h) not in live:
+                live["c", h] = shared([P, 4, HALF], F32, f"c{h}", "block", 3)
+            c = live["c", h][:, i, :]
+            cols = slice(HALF * h, HALF * h + HALF)
+            nc.vector.tensor_tensor(
+                out=c.rearrange("p (k u e) -> p k u e", u=2, e=2),
+                in0=live["correlation", h, i][:].rearrange("p (u k e) -> p k u e", u=2, e=2),
+                in1=tau_rows[:, cols].rearrange("p (k u e) -> p k u e", u=2, e=2),
+                op=MULT,
+            )
+            nc.sync.dma_start(out=out_1.rearrange("(p i) l -> p i l", i=4)[:, i, cols], in_=c)
 
         warm_up()
         warm_up()
+        turn_force(0, 0, 0)
+        turn_force(0, 0, 1)
+        quantise_force(0, 0, 0)
+        interleave_root(0, 0, on_vector)
         warm_up()
-        ft(0, 0)
-        ri(0, 0, "v")
-        fq(0, 0)
-        rq(0, 0)
+        interleave_root(1, 0, on_vector)
+        turn_force(0, 0, 2)
         warm_up()
-        ri(1, 0, "v")
-        ft(0, 1)
-        fq(0, 1)
-        ft(1, 0)
-        s1(0, 0, 0, 0)
-        ri(0, 1, "v")
-        s1(0, 0, 1, 0)
-        ri(1, 1, "s")
-        rq(1, 0)
-        rq(0, 1)
-        s1(0, 1, 0, 0)
-        s1(0, 0, 0, 1)
-        ri(0, 2, "v")
-        s1(0, 0, 1, 1)
-        rq(0, 2)
-        fq(1, 0)
-        ri(1, 2, "s")
-        s1(0, 0, 0, 2)
-        s1(0, 0, 1, 2)
-        rq(1, 1)
-        ya(0, 0, 0)
-        ft(1, 1)
-        rq(1, 2)
-        ya(0, 0, 1)
-        s1(0, 1, 0, 1)
-        s1(0, 1, 1, 0)
-        s1(0, 1, 0, 2)
-        s1(0, 1, 1, 1)
-        ya(0, 1, 0)
-        fq(1, 1)
-        yi(0, 0, "s")
-        s1(1, 1, 0, 0)
-        s1(0, 1, 1, 2)
-        yt(0, 0)
-        s1(1, 1, 0, 1)
-        ya(0, 1, 1)
-        s1(1, 0, 0, 0)
-        s1(1, 1, 0, 2)
-        yt(0, 1)
-        s1(1, 0, 0, 1)
-        yq(0, 0)
-        s1(1, 0, 1, 0)
-        s1(1, 0, 0, 2)
-        yi(0, 1, "s")
-        ya(1, 1, 0)
-        yk(0, 0)
-        s1(1, 0, 1, 1)
-        yk(0, 1)
-        s1(1, 1, 1, 0)
-        ya(1, 0, 0)
-        s1(1, 0, 1, 2)
-        yq(0, 1)
-        ya(1, 0, 1)
-        s1(1, 1, 1, 1)
-        yt(1, 0)
-        s1(1, 1, 1, 2)
-        ya(1, 1, 1)
-        s2(0, 0)
-        yi(1, 0, "v")
-        s2(0, 1)
-        yk(1, 0)
-        yq(1, 0)
-        yt(1, 1)
-        yi(1, 1, "v")
-        s2(0, 2)
-        yq(1, 1)
-        yk(1, 1)
-        ox(0)
-        s2(0, 3)
-        s2(1, 0, on_vector=(2,))
-        ox(1)
-        s2(1, 1, on_vector=(2,))
-        ot(0)
-        oq(0)
-        s2(1, 2, on_vector=(2,))
-        s2(1, 3, on_vector=(2,))
-        s3(0, 0)
-        ot(1)
-        co(0, 0)
-        oq(1)
-        s3(1, 0)
-        co(1, 0)
-        s3(0, 1)
-        s3(1, 1)
-        co(0, 1)
-        co(1, 1)
+        turn_force(0, 1, 0)
+        quantise_root(0, 0)
+        turn_force(0, 1, 1)
+        turn_force(0, 1, 2)
+        modes(0, 0, 0, 0)
+        quantise_force(0, 0, 1)
+        quantise_root(1, 0)
+        interleave_root(1, 1, on_vector)
+        quantise_force(0, 1, 0)
+        interleave_root(0, 1, on_scalar)
+        modes(0, 1, 0, 0)
+        turn_force(1, 0, 0)
+        quantise_force(0, 0, 2)
+        quantise_force(0, 1, 1)
+        quantise_root(1, 1)
+        quantise_root(0, 1)
+        turn_force(1, 0, 1)
+        interleave_root(0, 2, on_vector)
+        quantise_force(0, 1, 2)
+        modes(0, 0, 1, 0)
+        modes(0, 1, 0, 1)
+        modes(0, 0, 0, 1)
+        quantise_root(0, 2)
+        interleave_root(1, 2, on_scalar)
+        quantise_force(1, 0, 0)
+        modes(0, 0, 1, 1)
+        turn_force(1, 1, 0)
+        turn_force(1, 0, 2)
+        modes(0, 0, 0, 2)
+        modes(0, 0, 1, 2)
+        quantise_root(1, 2)
+        modes(0, 1, 0, 2)
+        quantise_force(1, 0, 1)
+        add_noise(0, 0, 0)
+        add_noise(0, 0, 1)
+        add_noise(0, 1, 0)
+        turn_force(1, 1, 1)
+        add_noise(0, 1, 1)
+        quantise_force(1, 1, 0)
+        turn_force(1, 1, 2)
+        modes(0, 1, 1, 0)
+        turn_y(0, 0)
+        add_noise(0, 0, 2)
+        turn_y(0, 1)
+        add_noise(0, 0, 3)
+        quantise_force(1, 1, 1)
+        modes(0, 1, 1, 1)
+        modes(1, 1, 0, 0)
+        modes(0, 1, 1, 2)
+        quantise_force(1, 0, 2)
+        modes(1, 1, 0, 1)
+        modes(1, 0, 0, 0)
+        quantise_force(1, 1, 2)
+        modes(1, 1, 0, 2)
+        add_noise(0, 1, 2)
+        add_noise(0, 1, 3)
+        add_noise(1, 1, 0)
+        modes(1, 0, 0, 1)
+        modes(1, 0, 1, 0)
+        modes(1, 0, 0, 2)
+        modes(1, 0, 1, 1)
+        add_noise(1, 1, 1)
+        interleave_y(0, 0, on_scalar)
+        modes(1, 1, 1, 0)
+        quantise_y_by_mode(0, 0)
+        interleave_y(0, 1, on_scalar)
+        modes(1, 0, 1, 2)
+        modes(1, 1, 1, 1)
+        add_noise(1, 0, 0)
+        add_noise(1, 0, 1)
+        turn_y(1, 0)
+        add_noise(1, 0, 2)
+        add_noise(1, 0, 3)
+        turn_y(0, 2)
+        displace(0, 0, split=True)
+        modes(1, 1, 1, 2)
+        turn_y(1, 1)
+        scale_obs(0)
+        add_noise(1, 1, 2)
+        turn_y(0, 3)
+        add_noise(1, 1, 3)
+        quantise_y_by_mode(1, 0)
+        interleave_y(1, 1, on_vector)
+        displace(0, 1)
+        order_obs(0, on_vector)
+        displace(1, 0)
+        quantise_y_by_mode(0, 1)
+        displace(1, 1, vector_chunk=1)
+        turn_y(1, 2)
+        scale_obs(1)
+        turn_y(1, 3)
+        displace(0, 2)
+        displace(0, 3, vector_chunk=0)
+        turn_obs(0)
+        turn_obs(1)
+        quantise_y_by_mode(1, 1)
+        interleave_y(1, 0, on_vector)
+        quantise_y_by_replica(0, 0)
+        quantise_y_by_replica(1, 0)
+        displace(1, 2, vector_chunk=0)
+        displace(1, 3)
+        quantise_obs(0)
+        correlate(0, 0)
+        order_obs(1, on_vector)
+        turn_obs(2)
+        turn_obs(3)
+        quantise_y_by_replica(1, 1)
+        quantise_y_by_replica(0, 1)
+        correlate(0, 1)
+        correlate(1, 0)
+        store_c(0, 0)
+        store_c(0, 1)
+        quantise_obs(1)
+        correlate(1, 1)
+        store_c(1, 0)
+        correlate(0, 2)
+        store_c(1, 1)
+        correlate(0, 3)
+        store_c(0, 2)
+        store_c(0, 3)
+        correlate(1, 2)
+        correlate(1, 3)
+        store_c(1, 2)
+        store_c(1, 3)

from contextlib import ExitStack

import concourse.mybir as mybir
from concourse.masks import make_identity

R, D, L, S = 1024, 1536, 1024, 512
P = 128
HALF = 512
K_PASS = 512
FLOPS = 2 * R * D * L + 2 * R * L * D + 2 * S * R * L

F32 = mybir.dt.float32
BF16 = mybir.dt.bfloat16
U32 = mybir.dt.uint32
I32 = mybir.dt.int32
U8 = mybir.dt.uint8
FP8 = mybir.dt.float8_e4m3fn
FP8X4 = mybir.dt.float8_e4m3fn_x4
FP4X4 = mybir.dt.float4_e2m1fn_x4
ADD = mybir.AluOpType.add
MULT = mybir.AluOpType.mult
COPY = mybir.ActivationFunctionType.Copy


def tile_brownian_mobility_step_s8_kernel(
    tc, force, root, noise, spread_words, spread_scales, obs_bytes, obs_scale, dt, tau, out_0, out_1
):
    nc = tc.nc
    with ExitStack() as ctx:
        ctx.enter_context(tc.manual_schedule())
        sbuf = ctx.enter_context(tc.tile_pool(name="sbuf", bufs=1))
        psum = ctx.enter_context(tc.psum_pool(name="psum", bufs=1))

        def own(shape, dtype, name):
            return sbuf.tile(shape, dtype, name=name, tag=name, align_bytes=64)

        def shared(shape, dtype, name, tag, bufs):
            return sbuf.tile(shape, dtype, name=name, tag=tag, bufs=bufs, align_bytes=64)

        def sums():
            return psum.tile([P, HALF], F32, name="sums", tag="sums", bufs=6)

        ident = own([P, P], F32, "ident")
        make_identity(nc, ident[:])
        zeros = own([P, HALF], BF16, "zeros")
        nc.vector.memset(zeros[:], 0.0)
        w_scales = own([P, 2, D], U8, "w_scales")
        nc.vector.memset(w_scales[:].rearrange("p g n -> p (g n)").bitcast(I32), 0)
        dt_in = own([P, 8], BF16, "dt_in")
        nc.gpsimd.dma_start(
            out=dt_in[:].rearrange("p (g t) -> p g t", t=4), in_=dt.rearrange("(g p t) -> p g t", p=P, t=4)
        )
        dt_f = own([P, 8], F32, "dt_f")
        nc.gpsimd.tensor_copy(out=dt_f[:], in_=dt_in[:])

        force_in = [[shared([P, 2, D], BF16, f"force{g}{a}", "row", 8) for a in range(2)] for g in range(2)]
        root_in = [shared([P, 4, L], BF16, f"root{p}", "block", 3) for p in range(3)]
        noise_in = [own([P, 4, L], BF16, f"noise{g}") for g in range(2)]
        obs_codes_in = own([P, 4 * R], U8, "obs_codes_in")
        scale_rows = own([P, R], F32, "scale_rows")
        tau_rows = own([P, L], BF16, "tau_rows")
        w = own([P, 2, 2 * D], U8, "w")

        def rows4(x, g):
            return x[K_PASS * g : K_PASS * (g + 1), :].rearrange("(p t) d -> p t d", t=4)

        def load_force(g, a):
            nc.sync.dma_start(out=force_in[g][a][:], in_=rows4(force, g)[:, 2 * a : 2 * a + 2, :])

        def load_root(p):
            nc.sync.dma_start(out=root_in[p][:], in_=rows4(root, p))

        def load_noise(g):
            nc.sync.dma_start(out=noise_in[g][:], in_=rows4(noise, g))

        def load_obs():
            nc.sync.dma_start(out=obs_codes_in[:], in_=obs_bytes.rearrange("(p i) r -> p (i r)", i=4))

        def load_scale():
            nc.sync.dma_start(out=scale_rows[:], in_=obs_scale.rearrange("o r -> (o r)").partition_broadcast(P))

        def load_tau():
            nc.sync.dma_start(out=tau_rows[:], in_=tau.partition_broadcast(P))

        def load_w_scales():
            for q in range(4):
                nc.sync.dma_start(
                    out=w_scales[32 * q : 32 * q + 4, :, :].bitcast(I32),
                    in_=spread_scales[:, 4 * q : 4 * q + 4, :].rearrange("g q n -> q g n").bitcast(I32),
                )

        def load_w():
            nc.sync.dma_start(out=w[:].bitcast(I32), in_=spread_words.rearrange("g p b -> p g b").bitcast(I32))

        for b in range(2):
            nc.sync.dma_start(out=force_in[0][0][:, b, :], in_=rows4(force, 0)[:, b, :])
        load_root(0)
        load_force(0, 1)
        load_root(1)
        load_force(1, 0)
        load_root(2)
        load_force(1, 1)
        load_noise(0)
        load_tau()
        load_noise(1)
        load_obs()
        load_scale()
        load_w()
        load_w_scales()

        force_q = [(own([P, 3, 512], U32, f"force_c{g}"), own([P, 3, 512], U8, f"force_s{g}")) for g in range(2)]
        root_q = [
            [(own([P, HALF], U32, f"root_c{h}{p}"), own([P, HALF], U8, f"root_s{h}{p}")) for p in range(3)]
            for h in range(2)
        ]
        y = [[own([P, 4, HALF], BF16, f"y{g}{h}") for h in range(2)] for g in range(2)]
        y_by_replica = [
            [(own([P, HALF], U32, f"yr_c{g}{h}"), own([P, HALF], U8, f"yr_s{g}{h}")) for h in range(2)]
            for g in range(2)
        ]
        y_by_mode = [
            [(own([P, 512], U32, f"ym_c{g}{a}"), own([P, 512], U8, f"ym_s{g}{a}")) for a in range(2)]
            for g in range(2)
        ]
        obs_q = [(own([P, 512], U32, f"obs_c{a}"), own([P, 512], U8, f"obs_s{a}")) for a in range(2)]
        obs = own([P, 4 * R], BF16, "obs")
        live = {}

        on_vector = nc.vector.tensor_copy
        on_scalar = nc.scalar.copy

        def quantise(key, codes, scales):
            nc.vector.quantize_mx(out=codes.bitcast(FP8X4), scales=scales, in_=live[key])

        def turn(out, blocks, step):
            bank = psum.tile([P, 2, 2, P], F32, name="turned", tag="turned", bufs=2)
            for b, (words, first) in enumerate(blocks):
                for u in range(2):
                    k = first + (u if step == 2 else P * u)
                    nc.tensor.transpose(bank[:, b, u, :], words[:, k : k + (P - 1) * step + 1 : step], ident[:])
            nc.scalar.copy(
                out=out.bitcast(F32).rearrange("p (b r u) -> p b r u", b=2, u=2),
                in_=bank[:].rearrange("p b u r -> p b r u"),
            )

        def half_of_pair(key, b):
            if key not in live:
                live[key] = shared([P, 2048], BF16, "pair", "pair", 4)[:]
            return live[key][:, 1024 * b : 1024 * b + 1024]

        def interleave(key, copy, rows):
            tile = shared([P, HALF, 4], BF16, "interleaved", "interleaved", 4)
            copy(
                out=tile[:].rearrange("p (c i) t -> p c t i", i=4),
                in_=rows.rearrange("p t (c i) -> p c t i", i=4),
            )
            live[key] = tile[:].rearrange("p c t -> p (c t)")

        def warm_up():
            bank = sums()
            for k in range(2):
                nc.tensor.matmul(bank[:], zeros[:, 0:P], zeros[:], start=True, stop=True)

        def turn_force(g, a, p):
            words = force_in[g][a][:].rearrange("p t d -> p (t d)").bitcast(F32)
            tile = shared([P, 1024], BF16, "force_turned", "force_turned", 6)
            turn(tile[:], [(words, D // 2 * b + 256 * p) for b in range(2)], 2)
            live["force", g, a, p] = tile[:]

        def quantise_force(g, a, p):
            codes, scales = force_q[g]
            tiles = slice(256 * a, 256 * a + 256)
            quantise(("force", g, a, p), codes[:, p, tiles], scales[:, p, tiles])

        def interleave_root(h, p, copy):
            interleave(("root", h, p), copy, root_in[p][:, :, HALF * h : HALF * h + HALF])

        def quantise_root(h, p):
            codes, scales = root_q[h][p]
            quantise(("root", h, p), codes[:], scales[:])

        def modes(g, h, a, p):
            f_codes, f_scales = force_q[g]
            r_codes, r_scales = root_q[h][p]
            for t in (2 * a, 2 * a + 1):
                if p == 0:
                    live["modes", g, h, t] = sums()
                m = slice(P * t, P * t + P)
                nc.tensor.matmul_mx(
                    out=live["modes", g, h, t][:],
                    lhsT=f_codes[:, p, m].bitcast(FP8X4),
                    lhsT_scale=f_scales[:, p, m],
                    rhs=r_codes[:].bitcast(FP8X4),
                    rhs_scale=r_scales[:],
                    start=(p == 0),
                    stop=(p == 2),
                )

        def add_noise(g, h, t):
            nc.vector.tensor_tensor(
                out=y[g][h][:, t, :].rearrange("p (u k e) -> p u k e", u=2, e=2),
                in0=live["modes", g, h, t][:].rearrange("p (k u e) -> p u k e", u=2, e=2),
                in1=noise_in[g][:, t, HALF * h : HALF * h + HALF].rearrange("p (k u e) -> p u k e", u=2, e=2),
                op=ADD,
            )

        def interleave_y(g, h, copy):
            interleave(("y", g, h), copy, y[g][h][:])

        def quantise_y_by_replica(g, h):
            codes, scales = y_by_replica[g][h]
            quantise(("y", g, h), codes[:], scales[:])

        def turn_y(g, t):
            halves = [(y[g][h][:].rearrange("p t c -> p (t c)").bitcast(F32), 256 * t) for h in range(2)]
            turn(half_of_pair(("turned y", g, t // 2), t % 2), halves, 1)

        def quantise_y_by_mode(g, a):
            codes, scales = y_by_mode[g][a]
            quantise(("turned y", g, a), codes[:], scales[:])

        def displace(g, t, vector_chunk=None, split=False):
            dx = shared([P, D], F32, f"dx{g}{t}", "row", 8)
            step = dt_f[:, 4 * g + t : 4 * g + t + 1]
            codes, scales = y_by_mode[g][t // 2]
            for n in range(3):
                bank = sums()
                cols = slice(HALF * n, HALF * n + HALF)
                for h in range(2):
                    m = slice(256 * (t % 2) + P * h, 256 * (t % 2) + P * h + P)
                    nc.tensor.matmul_mx(
                        out=bank[:],
                        lhsT=codes[:, m].bitcast(FP8X4),
                        lhsT_scale=scales[:, m],
                        rhs=w[:, h, 2 * HALF * n : 2 * HALF * (n + 1)].bitcast(FP4X4),
                        rhs_scale=w_scales[:, h, cols],
                        start=(h == 0),
                        stop=(h == 1),
                    )
                if n == vector_chunk:
                    nc.vector.tensor_scalar(out=dx[:, cols], in0=bank[:], scalar1=step, scalar2=None, op0=MULT)
                else:
                    nc.scalar.activation(out=dx[:, cols], in_=bank[:], func=COPY, scale=step)
                if split:
                    nc.sync.dma_start(out=rows4(out_0, g)[:, t, cols], in_=dx[:, cols])
            if not split:
                nc.sync.dma_start(out=rows4(out_0, g)[:, t, :], in_=dx[:])

        def scale_obs(a):
            for i in (2 * a, 2 * a + 1):
                cols = slice(R * i, R * (i + 1))
                nc.vector.tensor_tensor(
                    out=obs[:, cols], in0=obs_codes_in[:, cols].bitcast(FP8), in1=scale_rows[:], op=MULT
                )

        def order_obs(a, copy):
            if "obs" not in live:
                live["obs"] = shared([P, 2 * R], F32, "obs_words", "block", 3)
            words = slice(R * a, R * (a + 1))
            copy(
                out=live["obs"][:, words].rearrange("p (b u k) -> p b u k", u=2, k=P),
                in_=obs[:].bitcast(F32)[:, words].rearrange("p (b k u) -> p b u k", u=2, k=P),
            )

        def turn_obs(i):
            turn(half_of_pair(("turned obs", i // 2), i % 2), [(live["obs"], 512 * i + 256 * g) for g in range(2)], 1)

        def quantise_obs(a):
            codes, scales = obs_q[a]
            quantise(("turned obs", a), codes[:], scales[:])

        def correlate(h, i):
            bank = sums()
            codes, scales = obs_q[i // 2]
            for g in range(2):
                m = slice(256 * (i % 2) + P * g, 256 * (i % 2) + P * g + P)
                y_codes, y_scales = y_by_replica[g][h]
                nc.tensor.matmul_mx(
                    out=bank[:],
                    lhsT=codes[:, m].bitcast(FP8X4),
                    lhsT_scale=scales[:, m],
                    rhs=y_codes[:].bitcast(FP8X4),
                    rhs_scale=y_scales[:],
                    start=(g == 0),
                    stop=(g == 1),
                )
            live["correlation", h, i] = bank

        def store_c(h, i):
            if ("c", h) not in live:
                live["c", h] = shared([P, 4, HALF], F32, f"c{h}", "block", 3)
            c = live["c", h][:, i, :]
            cols = slice(HALF * h, HALF * h + HALF)
            nc.vector.tensor_tensor(
                out=c.rearrange("p (k u e) -> p k u e", u=2, e=2),
                in0=live["correlation", h, i][:].rearrange("p (u k e) -> p k u e", u=2, e=2),
                in1=tau_rows[:, cols].rearrange("p (k u e) -> p k u e", u=2, e=2),
                op=MULT,
            )
            nc.sync.dma_start(out=out_1.rearrange("(p i) l -> p i l", i=4)[:, i, cols], in_=c)

        warm_up()
        warm_up()
        turn_force(0, 0, 0)
        turn_force(0, 0, 1)
        quantise_force(0, 0, 0)
        interleave_root(0, 0, on_vector)
        warm_up()
        interleave_root(1, 0, on_vector)
        turn_force(0, 0, 2)
        warm_up()
        turn_force(0, 1, 0)
        quantise_root(0, 0)
        turn_force(0, 1, 1)
        turn_force(0, 1, 2)
        modes(0, 0, 0, 0)
        quantise_force(0, 0, 1)
        quantise_root(1, 0)
        interleave_root(1, 1, on_vector)
        quantise_force(0, 1, 0)
        interleave_root(0, 1, on_scalar)
        modes(0, 1, 0, 0)
        turn_force(1, 0, 0)
        quantise_force(0, 0, 2)
        quantise_force(0, 1, 1)
        quantise_root(1, 1)
        quantise_root(0, 1)
        turn_force(1, 0, 1)
        interleave_root(0, 2, on_vector)
        quantise_force(0, 1, 2)
        modes(0, 0, 1, 0)
        modes(0, 1, 0, 1)
        modes(0, 0, 0, 1)
        quantise_root(0, 2)
        interleave_root(1, 2, on_scalar)
        quantise_force(1, 0, 0)
        modes(0, 0, 1, 1)
        turn_force(1, 1, 0)
        turn_force(1, 0, 2)
        modes(0, 0, 0, 2)
        modes(0, 0, 1, 2)
        quantise_root(1, 2)
        modes(0, 1, 0, 2)
        quantise_force(1, 0, 1)
        add_noise(0, 0, 0)
        add_noise(0, 0, 1)
        add_noise(0, 1, 0)
        turn_force(1, 1, 1)
        add_noise(0, 1, 1)
        quantise_force(1, 1, 0)
        turn_force(1, 1, 2)
        modes(0, 1, 1, 0)
        turn_y(0, 0)
        add_noise(0, 0, 2)
        turn_y(0, 1)
        add_noise(0, 0, 3)
        quantise_force(1, 1, 1)
        modes(0, 1, 1, 1)
        modes(1, 1, 0, 0)
        modes(0, 1, 1, 2)
        quantise_force(1, 0, 2)
        modes(1, 1, 0, 1)
        modes(1, 0, 0, 0)
        quantise_force(1, 1, 2)
        modes(1, 1, 0, 2)
        add_noise(0, 1, 2)
        add_noise(0, 1, 3)
        add_noise(1, 1, 0)
        modes(1, 0, 0, 1)
        modes(1, 0, 1, 0)
        modes(1, 0, 0, 2)
        modes(1, 0, 1, 1)
        add_noise(1, 1, 1)
        interleave_y(0, 0, on_scalar)
        modes(1, 1, 1, 0)
        quantise_y_by_mode(0, 0)
        interleave_y(0, 1, on_scalar)
        modes(1, 0, 1, 2)
        modes(1, 1, 1, 1)
        add_noise(1, 0, 0)
        add_noise(1, 0, 1)
        turn_y(1, 0)
        add_noise(1, 0, 2)
        add_noise(1, 0, 3)
        turn_y(0, 2)
        displace(0, 0, split=True)
        modes(1, 1, 1, 2)
        turn_y(1, 1)
        scale_obs(0)
        add_noise(1, 1, 2)
        turn_y(0, 3)
        add_noise(1, 1, 3)
        quantise_y_by_mode(1, 0)
        interleave_y(1, 1, on_vector)
        displace(0, 1)
        order_obs(0, on_vector)
        displace(1, 0)
        quantise_y_by_mode(0, 1)
        displace(1, 1, vector_chunk=1)
        turn_y(1, 2)
        scale_obs(1)
        turn_y(1, 3)
        displace(0, 2)
        displace(0, 3, vector_chunk=0)
        turn_obs(0)
        turn_obs(1)
        quantise_y_by_mode(1, 1)
        interleave_y(1, 0, on_vector)
        quantise_y_by_replica(0, 0)
        quantise_y_by_replica(1, 0)
        displace(1, 2, vector_chunk=0)
        displace(1, 3)
        quantise_obs(0)
        correlate(0, 0)
        order_obs(1, on_vector)
        turn_obs(2)
        turn_obs(3)
        quantise_y_by_replica(1, 1)
        quantise_y_by_replica(0, 1)
        correlate(0, 1)
        correlate(1, 0)
        store_c(0, 0)
        store_c(0, 1)
        quantise_obs(1)
        correlate(1, 1)
        store_c(1, 0)
        correlate(0, 2)
        store_c(1, 1)
        correlate(0, 3)
        store_c(0, 2)
        store_c(0, 3)
        correlate(1, 2)
        correlate(1, 3)
        store_c(1, 2)
        store_c(1, 3)
